import numpy as np
import ml_dtypes


def mxq(x, axis, fmt="e4m3"):
    dtype, down = {"e4m3": (ml_dtypes.float8_e4m3fn, 7), "e5m2": (ml_dtypes.float8_e5m2, 14)}[fmt]
    v = np.moveaxis(np.asarray(x, np.float32).astype(ml_dtypes.bfloat16).astype(np.float64), axis, -1)
    blocks = v.reshape(v.shape[:-1] + (-1, 32))
    amax = np.abs(blocks).max(-1, keepdims=True)
    byte = np.maximum(np.where(amax > 0, np.frexp(amax)[1] - 1 + 127, 0) - down, 1)
    scale = np.exp2(byte - 127.0)
    codes = (blocks / scale).astype(np.float32).astype(dtype).astype(np.float64)
    return np.moveaxis((codes * scale).reshape(v.shape), -1, axis)


WIDE = False


def mx_kscale(k):
    if not WIDE:
        return np.ones(k)
    levels = np.array([10, -10, 5, -5, 0])
    if k % 512:
        return np.exp2(np.random.permutation(np.resize(levels, k // 32))).repeat(32)
    a = np.empty((k // 512, 16))
    for p in range(k // 512):
        a[p, :8] = np.random.permutation(np.resize(levels, 8))
        for g in range(8):
            far = levels[np.abs(levels - a[p, g]) >= 10]
            a[p, g + 8] = far[np.random.randint(len(far))]
    return np.exp2(a.ravel()).repeat(32)


def f64(x):
    return np.asarray(x).astype(np.float64)


def striped(idx):
    return np.tile(idx.reshape(-1, 16).T, (8, 1)).astype(np.uint16)


def unstriped(offs):
    return offs[:16].T.reshape(-1).astype(np.int64)


def pack_weight(w):
    k, n = w.shape
    w = f64(np.asarray(w, np.float32).astype(ml_dtypes.bfloat16)).reshape(k // 32, 32, n)
    amax = np.abs(w).max(1)
    byte = np.clip(np.where(amax > 0, np.frexp(amax)[1] - 1 + 127 - 7, 1), 1, 254)
    scaled = (w * np.exp2(127.0 - byte)[:, None, :]).reshape(k, n).astype(np.float32)
    words = np.ascontiguousarray(scaled.reshape(k // 512, 128, 4, n).transpose(0, 1, 3, 2)).astype(ml_dtypes.float8_e4m3fn).view(np.uint8)
    return words, np.ascontiguousarray(byte.astype(np.uint8).reshape(k // 512, 16, n))


def unpack_weight(words, scales):
    g, p, n, _ = words.shape
    vals = np.ascontiguousarray(words).view(ml_dtypes.float8_e4m3fn).astype(np.float64) * np.repeat(np.exp2(scales.astype(np.float64) - 127.0), 8, axis=1)[..., None]
    return vals.transpose(0, 1, 3, 2).reshape(g * 512, n)


def sigmoid(v):
    return 1.0 / (1.0 + np.exp(-np.maximum(v, -700.0)))


def gelu(v):
    return 0.5 * v * (1.0 + np.tanh(np.sqrt(2.0 / np.pi) * (v + 0.044715 * v**3)))


K, T, S, V, H, W = 512, 2048, 512, 512, 512, 1024


def setup_inputs():
    n = np.random.standard_normal
    s = mx_kscale(K)[:, None]
    u = mx_kscale(H)
    packed_xT = pack_weight(n((K, T)) * s)
    packed_eT = pack_weight(n((K, W)) / np.sqrt(2 * K) / s)
    return {
        "x_words": packed_xT[0],
        "x_scales": packed_xT[1],
        "e_words": packed_eT[0],
        "e_scales": packed_eT[1],
        "w1": (n((K, H)) / np.sqrt(K) / s * u).astype(np.float32),
        "w2": (n((K, H)) / np.sqrt(K) * np.sqrt(2 * K) * s / u / np.sqrt(2 * H)).astype(np.float32),
        "offs": striped(np.random.permutation(T)[:S]),
        "cand": striped(np.random.permutation(W)[:V]),
    }


def reference(x_words, x_scales, e_words, e_scales, w1, w2, offs, cand):
    xq = unpack_weight(x_words, x_scales)[:, unstriped(offs)]
    p = gelu(mxq(f64(w1), 0, "e4m3").T @ xq)
    e_cand = unpack_weight(e_words, e_scales)[:, unstriped(cand)]
    d = gelu(mxq(f64(w2), 0, "e4m3").T @ e_cand)
    y = mxq(p, 0, "e4m3").T @ mxq(d, 0, "e4m3") + xq.T @ e_cand
    return sigmoid(y)

@@ -1,0 +1,184 @@
+from contextlib import ExitStack
+
+import concourse.mybir as mybir
+
+F32 = mybir.dt.float32
+BF16 = mybir.dt.bfloat16
+I32 = mybir.dt.int32
+U32 = mybir.dt.uint32
+U16 = mybir.dt.uint16
+U8 = mybir.dt.uint8
+FP8X4 = mybir.dt.float8_e4m3fn_x4
+GELU = mybir.ActivationFunctionType.Gelu_apprx_tanh
+TANH = mybir.ActivationFunctionType.Tanh
+MULT = mybir.AluOpType.mult
+ADD = mybir.AluOpType.add
+
+P = 128
+PACK = 4
+K = 512
+USERS = 2048
+ITEMS = 1024
+PICKED = 512
+CHUNK = 128
+CHUNKS = PICKED // CHUNK
+X_PIECE = 256
+
+FLOPS = 4 * 2 * K * PICKED * PICKED
+
+
+def tile_picked_zneumf_gelu_p_kernel(
+    tc, x_words, x_scales, e_words, e_scales, w1, w2, offs, cand, out
+):
+    nc = tc.nc
+    with ExitStack() as ctx:
+        keep = ctx.enter_context(tc.tile_pool(name="keep", bufs=1))
+        tower_psum = ctx.enter_context(tc.psum_pool(name="tower_psum", bufs=4))
+        score_psum = ctx.enter_context(tc.psum_pool(name="score_psum", bufs=1))
+
+        offs_sb = keep.tile([P, PICKED // 16], U16, name="offs_sb")
+        cand_sb = keep.tile([P, PICKED // 16], U16, name="cand_sb")
+        e_tab = keep.tile([P, ITEMS], U32, name="e_tab", align_bytes=64)
+        xs_tab = keep.tile([P, USERS], U8, name="xs_tab", align_bytes=64)
+        es_tab = keep.tile([P, ITEMS], U8, name="es_tab", align_bytes=64)
+        w2_raw = keep.tile([P, PACK * K], F32, name="w2_raw", tag="w2_slot", align_bytes=64)
+        warm_in = keep.tile([P, 1], F32, name="warm_in", tag="w1_slot", align_bytes=64)
+        warm_out = keep.tile([P, 1], F32, name="warm_out", tag="x_slot", align_bytes=64)
+
+        nc.vector.memset(es_tab[:].bitcast(I32), 0)
+        nc.gpsimd.memset(xs_tab[:].bitcast(I32), 0)
+        nc.vector.memset(warm_in[:], 0.0)
+        nc.scalar.activation(warm_out[:], warm_in[:], GELU)
+
+        nc.sync.dma_start(cand_sb[:], cand)
+        nc.sync.dma_start(offs_sb[:], offs)
+        nc.sync.dma_start(e_tab[:].bitcast(I32), e_words[0].rearrange("p n t -> p (n t)").bitcast(I32))
+        for r in range(4):
+            nc.sync.dma_start(es_tab[r:P:32, :].bitcast(I32), e_scales[0][r:16:4, :].bitcast(I32))
+        nc.sync.dma_start(w2_raw[:], w2.rearrange("(p j) c -> p (j c)", j=PACK))
+        for r in range(4):
+            nc.sync.dma_start(xs_tab[r:P:32, :].bitcast(I32), x_scales[0][r:16:4, :].bitcast(I32))
+        w1_raw = keep.tile([P, PACK * K], F32, name="w1_raw", tag="w1_slot", align_bytes=64)
+        x_tab = keep.tile([P, USERS], U32, name="x_tab", tag="x_slot", align_bytes=64)
+        nc.sync.dma_start(w1_raw[:], w1.rearrange("(p j) c -> p (j c)", j=PACK))
+        nc.sync.dma_start(x_tab[:].bitcast(I32), x_words[0].rearrange("p n t -> p (n t)").bitcast(I32))
+
+
+        e_codes = keep.tile([P, PICKED], U32, name="e_codes", align_bytes=64)
+        e_sc = keep.tile([P, PICKED], U8, name="e_sc", align_bytes=64)
+
+        def weight_tiles(name, tag, codes_tag):
+            grouped = keep.tile([P, PACK * K], BF16, name=name + "_grouped", tag=tag, align_bytes=64)
+            codes = keep.tile([P, K], U32, name=name + "_codes", tag=codes_tag, align_bytes=64)
+            scales = keep.tile([P, K], U8, name=name + "_scales", align_bytes=64)
+            return grouped, codes, scales
+
+        def cast_views(raw, grouped):
+            src = raw[:].rearrange("p (j q t i) -> p t q j i", j=PACK, t=PACK, i=4)
+            dst = grouped[:].rearrange("p (t q i j) -> p t q j i", j=PACK, t=PACK, i=4)
+            return src, dst
+
+        def quantize(grouped, codes, scales, c0, c1):
+            nc.vector.quantize_mx(
+                out=codes[:, c0:c1].bitcast(FP8X4),
+                scales=scales[:, c0:c1],
+                in_=grouped[:, PACK * c0 : PACK * c1],
+            )
+
+        def tower_matmuls(w_codes, w_scales, codes, scales, c):
+            cols = slice(c * CHUNK, (c + 1) * CHUNK)
+            bank = tower_psum.tile([P, PACK, CHUNK], F32, name="tower_bank")
+            for t in range(PACK):
+                wc = slice(t * P, (t + 1) * P)
+                nc.tensor.matmul_mx(
+                    out=bank[:, t, :],
+                    lhsT=w_codes[:, wc].bitcast(FP8X4),
+                    lhsT_scale=w_scales[:, wc],
+                    rhs=codes[:, cols].bitcast(FP8X4),
+                    rhs_scale=scales[:, cols],
+                    start=True,
+                    stop=True,
+                )
+            return bank
+
+        def gelu(bank, hidden, c):
+            dst = hidden[:, PACK * c * CHUNK : PACK * (c + 1) * CHUNK].rearrange("p (n t) -> p n t", t=PACK)
+            nc.scalar.activation(dst, bank[:].rearrange("p t n -> p n t"), GELU)
+
+        nc.vector.tensor_copy(e_codes[:], e_tab[:].indirect(cand_sb[:]))
+        nc.vector.tensor_copy(e_sc[:], es_tab[:].indirect(cand_sb[:]))
+
+        w2_grouped, w2_codes, w2_scales = weight_tiles("w2", "stage", "w2_codes")
+        src, dst = cast_views(w2_raw, w2_grouped)
+        nc.vector.tensor_copy(dst[:, 0:2], src[:, 0:2])
+        nc.scalar.copy(dst[:, 2], src[:, 2])
+        nc.scalar.copy(dst[:, 3], src[:, 3])
+        for t in range(PACK):
+            quantize(w2_grouped, w2_codes, w2_scales, t * P, (t + 1) * P)
+
+        x_sc = keep.tile([P, PICKED], U8, name="x_sc", tag="w2_slot", align_bytes=64)
+        nc.vector.tensor_copy(x_sc[:], xs_tab[:].indirect(offs_sb[:]))
+
+        d_hidden = keep.tile([P, PACK * K], BF16, name="d_hidden", align_bytes=64)
+        for c in range(CHUNKS):
+            bank = tower_matmuls(w2_codes, w2_scales, e_codes, e_sc, c)
+            gelu(bank, d_hidden, c)
+
+        w1_grouped, w1_codes, w1_scales = weight_tiles("w1", "stage", "w1_codes")
+        src, dst = cast_views(w1_raw, w1_grouped)
+        nc.vector.tensor_copy(dst[:, 0:2], src[:, 0:2])
+        nc.vector.tensor_copy(dst[:, 2:4], src[:, 2:4])
+        quantize(w1_grouped, w1_codes, w1_scales, 0, 256)
+        quantize(w1_grouped, w1_codes, w1_scales, 256, 512)
+        for t in range(PACK):
+            wc = slice(t * P, (t + 1) * P)
+            spare = tower_psum.tile([P, PACK, CHUNK], F32, name="tower_bank")
+            nc.tensor.matmul_mx(
+                out=spare[:].rearrange("p t n -> p (t n)"),
+                lhsT=w1_codes[:, wc].bitcast(FP8X4),
+                lhsT_scale=w1_scales[:, wc],
+                rhs=e_codes[:].bitcast(FP8X4),
+                rhs_scale=e_sc[:],
+                start=True,
+                stop=True,
+            )
+
+        x_codes = keep.tile([P, PICKED], U32, name="x_codes", tag="stage", align_bytes=64)
+        for g in range(PICKED // X_PIECE):
+            nc.vector.tensor_copy(
+                x_codes[:, g * X_PIECE : (g + 1) * X_PIECE],
+                x_tab[:].indirect(offs_sb[:, g * X_PIECE // 16 : (g + 1) * X_PIECE // 16]),
+            )
+        d_codes = keep.tile([P, K], U32, name="d_codes", tag="x_slot", align_bytes=64)
+        d_scales = keep.tile([P, K], U8, name="d_scales", align_bytes=64)
+        quantize(d_hidden, d_codes, d_scales, 0, 256)
+        quantize(d_hidden, d_codes, d_scales, 256, 512)
+
+        p_hidden, p_codes, p_scales = weight_tiles("p", "p_hidden", "p_codes")
+        scores = [score_psum.tile([P, PICKED], F32, name="score%d" % c) for c in range(CHUNKS)]
+
+        def score_pass(c, l_codes, l_scales, r_codes, r_scales, first):
+            cols = slice(c * CHUNK, (c + 1) * CHUNK)
+            nc.tensor.matmul_mx(
+                out=scores[c][:],
+                lhsT=l_codes[:, cols].bitcast(FP8X4),
+                lhsT_scale=l_scales[:, cols],
+                rhs=r_codes[:].bitcast(FP8X4),
+                rhs_scale=r_scales[:],
+                start=first,
+                stop=not first,
+            )
+
+        for c in range(CHUNKS):
+            bank = tower_matmuls(w1_codes, w1_scales, x_codes, x_sc, c)
+            gelu(bank, p_hidden, c)
+            quantize(p_hidden, p_codes, p_scales, c * CHUNK, (c + 1) * CHUNK)
+
+        for c in range(CHUNKS):
+            score_pass(c, x_codes, x_sc, e_codes, e_sc, True)
+            score_pass(c, p_codes, p_scales, d_codes, d_scales, False)
+            half = keep.tile([P, PICKED], F32, name="half%d" % c)
+            res = keep.tile([P, PICKED], F32, name="res%d" % c)
+            nc.scalar.activation(half[:], scores[c][:], TANH, scale=0.5)
+            nc.vector.tensor_scalar(res[:], half[:], 0.5, 0.5, MULT, ADD)
+            nc.sync.dma_start(out[c * CHUNK : (c + 1) * CHUNK, :], res[:])

@@ -23,6 +23,7 @@ PICKED = 512
 CHUNK = 128
 CHUNKS = PICKED // CHUNK
 X_PIECE = 256
+E_ROW = 4
 
 FLOPS = 4 * 2 * K * PICKED * PICKED
 
@@ -39,7 +40,7 @@ def tile_picked_zneumf_gelu_p_kernel(
         offs_sb = keep.tile([P, PICKED // 16], U16, name="offs_sb")
         cand_sb = keep.tile([P, PICKED // 16], U16, name="cand_sb")
         e_tab = keep.tile([P, ITEMS], U32, name="e_tab", align_bytes=64)
-        xs_tab = keep.tile([P, USERS], U8, name="xs_tab", align_bytes=64)
+        xs_tab = keep.tile([P, USERS], U8, name="xs_tab", tag="xs_slot", align_bytes=64)
         es_tab = keep.tile([P, ITEMS], U8, name="es_tab", align_bytes=64)
         w2_raw = keep.tile([P, PACK * K], F32, name="w2_raw", tag="w2_slot", align_bytes=64)
         warm_in = keep.tile([P, 1], F32, name="warm_in", tag="w1_slot", align_bytes=64)
@@ -54,7 +55,7 @@ def tile_picked_zneumf_gelu_p_kernel(
         nc.sync.dma_start(offs_sb[:], offs)
         nc.sync.dma_start(e_tab[:].bitcast(I32), e_words[0].rearrange("p n t -> p (n t)").bitcast(I32))
         for r in range(4):
-            nc.sync.dma_start(es_tab[r:P:32, :].bitcast(I32), e_scales[0][r:16:4, :].bitcast(I32))
+            nc.sync.dma_start(es_tab[E_ROW + r : P : 32, :].bitcast(I32), e_scales[0][r:16:4, :].bitcast(I32))
         nc.sync.dma_start(w2_raw[:], w2.rearrange("(p j) c -> p (j c)", j=PACK))
         for r in range(4):
             nc.sync.dma_start(xs_tab[r:P:32, :].bitcast(I32), x_scales[0][r:16:4, :].bitcast(I32))
@@ -85,7 +86,7 @@ def tile_picked_zneumf_gelu_p_kernel(
                 in_=grouped[:, PACK * c0 : PACK * c1],
             )
 
-        def tower_matmuls(w_codes, w_scales, codes, scales, c):
+        def tower_matmuls(w_codes, w_scales, codes, scales, row, c):
             cols = slice(c * CHUNK, (c + 1) * CHUNK)
             bank = tower_psum.tile([P, PACK, CHUNK], F32, name="tower_bank")
             for t in range(PACK):
@@ -95,7 +96,7 @@ def tile_picked_zneumf_gelu_p_kernel(
                     lhsT=w_codes[:, wc].bitcast(FP8X4),
                     lhsT_scale=w_scales[:, wc],
                     rhs=codes[:, cols].bitcast(FP8X4),
-                    rhs_scale=scales[:, cols],
+                    rhs_scale=scales[row:P, cols],
                     start=True,
                     stop=True,
                 )
@@ -108,20 +109,21 @@ def tile_picked_zneumf_gelu_p_kernel(
         nc.vector.tensor_copy(e_codes[:], e_tab[:].indirect(cand_sb[:]))
         nc.vector.tensor_copy(e_sc[:], es_tab[:].indirect(cand_sb[:]))
 
-        w2_grouped, w2_codes, w2_scales = weight_tiles("w2", "stage", "w2_codes")
+        w2_grouped = keep.tile([P, PACK * K], BF16, name="w2_grouped", tag="stage", align_bytes=64)
         src, dst = cast_views(w2_raw, w2_grouped)
-        nc.vector.tensor_copy(dst[:, 0:2], src[:, 0:2])
-        nc.scalar.copy(dst[:, 2], src[:, 2])
-        nc.scalar.copy(dst[:, 3], src[:, 3])
+        nc.vector.tensor_copy(dst[:, 0], src[:, 0])
+        for t in range(1, PACK):
+            nc.scalar.copy(dst[:, t], src[:, t])
+        x_sc = keep.tile([P, PICKED], U8, name="x_sc", align_bytes=64)
+        nc.vector.tensor_copy(x_sc[:], xs_tab[:].indirect(offs_sb[:]))
+        w2_codes = keep.tile([P, K], U32, name="w2_codes", tag="xs_slot", align_bytes=64)
+        w2_scales = keep.tile([P, K], U8, name="w2_scales", align_bytes=64)
         for t in range(PACK):
             quantize(w2_grouped, w2_codes, w2_scales, t * P, (t + 1) * P)
 
-        x_sc = keep.tile([P, PICKED], U8, name="x_sc", tag="w2_slot", align_bytes=64)
-        nc.vector.tensor_copy(x_sc[:], xs_tab[:].indirect(offs_sb[:]))
-
         d_hidden = keep.tile([P, PACK * K], BF16, name="d_hidden", align_bytes=64)
         for c in range(CHUNKS):
-            bank = tower_matmuls(w2_codes, w2_scales, e_codes, e_sc, c)
+            bank = tower_matmuls(w2_codes, w2_scales, e_codes, e_sc, E_ROW, c)
             gelu(bank, d_hidden, c)
 
         w1_grouped, w1_codes, w1_scales = weight_tiles("w1", "stage", "w1_codes")
@@ -130,18 +132,6 @@ def tile_picked_zneumf_gelu_p_kernel(
         nc.vector.tensor_copy(dst[:, 2:4], src[:, 2:4])
         quantize(w1_grouped, w1_codes, w1_scales, 0, 256)
         quantize(w1_grouped, w1_codes, w1_scales, 256, 512)
-        for t in range(PACK):
-            wc = slice(t * P, (t + 1) * P)
-            spare = tower_psum.tile([P, PACK, CHUNK], F32, name="tower_bank")
-            nc.tensor.matmul_mx(
-                out=spare[:].rearrange("p t n -> p (t n)"),
-                lhsT=w1_codes[:, wc].bitcast(FP8X4),
-                lhsT_scale=w1_scales[:, wc],
-                rhs=e_codes[:].bitcast(FP8X4),
-                rhs_scale=e_sc[:],
-                start=True,
-                stop=True,
-            )
 
         x_codes = keep.tile([P, PICKED], U32, name="x_codes", tag="stage", align_bytes=64)
         for g in range(PICKED // X_PIECE):
@@ -164,21 +154,33 @@ def tile_picked_zneumf_gelu_p_kernel(
                 lhsT=l_codes[:, cols].bitcast(FP8X4),
                 lhsT_scale=l_scales[:, cols],
                 rhs=r_codes[:].bitcast(FP8X4),
-                rhs_scale=r_scales[:],
+                rhs_scale=r_scales,
                 start=first,
                 stop=not first,
             )
 
-        for c in range(CHUNKS):
-            bank = tower_matmuls(w1_codes, w1_scales, x_codes, x_sc, c)
+        def user_tower(c):
+            bank = tower_matmuls(w1_codes, w1_scales, x_codes, x_sc, 0, c)
             gelu(bank, p_hidden, c)
             quantize(p_hidden, p_codes, p_scales, c * CHUNK, (c + 1) * CHUNK)
 
-        for c in range(CHUNKS):
-            score_pass(c, x_codes, x_sc, e_codes, e_sc, True)
-            score_pass(c, p_codes, p_scales, d_codes, d_scales, False)
-            half = keep.tile([P, PICKED], F32, name="half%d" % c)
-            res = keep.tile([P, PICKED], F32, name="res%d" % c)
-            nc.scalar.activation(half[:], scores[c][:], TANH, scale=0.5)
-            nc.vector.tensor_scalar(res[:], half[:], 0.5, 0.5, MULT, ADD)
-            nc.sync.dma_start(out[c * CHUNK : (c + 1) * CHUNK, :], res[:])
+        def finish(c, pieces):
+            score_pass(c, x_codes, x_sc, e_codes, e_sc[E_ROW:P, :], True)
+            score_pass(c, p_codes, p_scales, d_codes, d_scales[:], False)
+            width = PICKED // pieces
+            for h in range(pieces):
+                cols = slice(h * width, (h + 1) * width)
+                half = keep.tile([P, width], F32, name="half%d_%d" % (c, h))
+                res = keep.tile([P, width], F32, name="res%d_%d" % (c, h))
+                nc.scalar.activation(half[:], scores[c][:, cols], TANH, scale=0.5)
+                nc.vector.tensor_scalar(res[:], half[:], 0.5, 0.5, MULT, ADD)
+                nc.sync.dma_start(out[c * CHUNK : (c + 1) * CHUNK, cols], res[:])
+
+        user_tower(0)
+        user_tower(1)
+        user_tower(2)
+        finish(0, 1)
+        user_tower(3)
+        finish(1, 1)
+        finish(2, 1)
+        finish(3, 2)

@@ -16,16 +16,21 @@ ADD = mybir.AluOpType.add
 
 P = 128
 PACK = 4
+RUN = 4
+QUADRANT = 32
+SCALE_ROWS = 16
+LIST_ROWS = 16
 K = 512
+HIDDEN = 512
 USERS = 2048
 ITEMS = 1024
 PICKED = 512
 CHUNK = 128
 CHUNKS = PICKED // CHUNK
-X_PIECE = 256
-E_ROW = 4
+HALF = PICKED // 2
+ITEM_SCALE_ROW = 4
 
-FLOPS = 4 * 2 * K * PICKED * PICKED
+FLOPS = 2 * PICKED * (2 * K * HIDDEN + HIDDEN * PICKED + K * PICKED)
 
 
 def tile_picked_zneumf_gelu_p_kernel(
@@ -34,153 +39,157 @@ def tile_picked_zneumf_gelu_p_kernel(
     nc = tc.nc
     with ExitStack() as ctx:
         keep = ctx.enter_context(tc.tile_pool(name="keep", bufs=1))
-        tower_psum = ctx.enter_context(tc.psum_pool(name="tower_psum", bufs=4))
+        tower_psum = ctx.enter_context(tc.psum_pool(name="tower_psum", bufs=CHUNKS))
         score_psum = ctx.enter_context(tc.psum_pool(name="score_psum", bufs=1))
 
-        offs_sb = keep.tile([P, PICKED // 16], U16, name="offs_sb")
-        cand_sb = keep.tile([P, PICKED // 16], U16, name="cand_sb")
-        e_tab = keep.tile([P, ITEMS], U32, name="e_tab", align_bytes=64)
-        xs_tab = keep.tile([P, USERS], U8, name="xs_tab", tag="xs_slot", align_bytes=64)
-        es_tab = keep.tile([P, ITEMS], U8, name="es_tab", align_bytes=64)
-        w2_raw = keep.tile([P, PACK * K], F32, name="w2_raw", tag="w2_slot", align_bytes=64)
-        warm_in = keep.tile([P, 1], F32, name="warm_in", tag="w1_slot", align_bytes=64)
-        warm_out = keep.tile([P, 1], F32, name="warm_out", tag="x_slot", align_bytes=64)
+        def mx_tile(shape, dtype, name, tag):
+            return keep.tile(shape, dtype, name=name, tag=tag, align_bytes=64)
 
-        nc.vector.memset(es_tab[:].bitcast(I32), 0)
-        nc.gpsimd.memset(xs_tab[:].bitcast(I32), 0)
-        nc.vector.memset(warm_in[:], 0.0)
-        nc.scalar.activation(warm_out[:], warm_in[:], GELU)
+        offs_sb = keep.tile([P, PICKED // LIST_ROWS], U16, name="offs_sb")
+        cand_sb = keep.tile([P, PICKED // LIST_ROWS], U16, name="cand_sb")
+        e_table = mx_tile([P, ITEMS], U32, "e_table", "e_table")
+        x_scale_table = mx_tile([P, USERS], U8, "x_scale_table", "x_scale_table_then_w2_codes")
+        e_scale_table = mx_tile([P, ITEMS], U8, "e_scale_table", "e_scale_table")
+        w2_raw = mx_tile([P, PACK * HIDDEN], F32, "w2_raw", "w2_raw")
+        zero_in = keep.tile([P, 1], F32, name="zero_in")
+        zero_bias = keep.tile([P, 1], F32, name="zero_bias")
 
+        nc.vector.memset(e_scale_table[:].bitcast(I32), 0)
+        nc.gpsimd.memset(x_scale_table[:].bitcast(I32), 0)
+        nc.vector.memset(zero_in[:], 0.0)
+        nc.scalar.activation(zero_bias[:], zero_in[:], GELU)
+
+        def load_words(table, words):
+            nc.sync.dma_start(table[:].bitcast(I32), words[0].rearrange("p n j -> p (n j)").bitcast(I32))
+
+        def load_scale_rows(table, scales, first_row):
+            rows_per_quadrant = SCALE_ROWS * QUADRANT // P
+            for r in range(rows_per_quadrant):
+                nc.sync.dma_start(
+                    table[first_row + r : P : QUADRANT, :].bitcast(I32),
+                    scales[0][r:SCALE_ROWS:rows_per_quadrant, :].bitcast(I32),
+                )
+
+        def load_weight(raw, w):
+            nc.sync.dma_start(raw[:], w.rearrange("(p j) c -> p (j c)", j=PACK))
+
+        load_words(e_table, e_words)
         nc.sync.dma_start(cand_sb[:], cand)
         nc.sync.dma_start(offs_sb[:], offs)
-        nc.sync.dma_start(e_tab[:].bitcast(I32), e_words[0].rearrange("p n t -> p (n t)").bitcast(I32))
-        for r in range(4):
-            nc.sync.dma_start(es_tab[E_ROW + r : P : 32, :].bitcast(I32), e_scales[0][r:16:4, :].bitcast(I32))
-        nc.sync.dma_start(w2_raw[:], w2.rearrange("(p j) c -> p (j c)", j=PACK))
-        for r in range(4):
-            nc.sync.dma_start(xs_tab[r:P:32, :].bitcast(I32), x_scales[0][r:16:4, :].bitcast(I32))
-        w1_raw = keep.tile([P, PACK * K], F32, name="w1_raw", tag="w1_slot", align_bytes=64)
-        x_tab = keep.tile([P, USERS], U32, name="x_tab", tag="x_slot", align_bytes=64)
-        nc.sync.dma_start(w1_raw[:], w1.rearrange("(p j) c -> p (j c)", j=PACK))
-        nc.sync.dma_start(x_tab[:].bitcast(I32), x_words[0].rearrange("p n t -> p (n t)").bitcast(I32))
+        load_scale_rows(e_scale_table, e_scales, ITEM_SCALE_ROW)
+        load_weight(w2_raw, w2)
+        load_scale_rows(x_scale_table, x_scales, 0)
+        w1_raw = mx_tile([P, PACK * HIDDEN], F32, "w1_raw", "w1_raw")
+        x_table = mx_tile([P, USERS], U32, "x_table", "x_table_then_d_codes")
+        load_weight(w1_raw, w1)
+        load_words(x_table, x_words)
 
-
-        e_codes = keep.tile([P, PICKED], U32, name="e_codes", align_bytes=64)
-        e_sc = keep.tile([P, PICKED], U8, name="e_sc", align_bytes=64)
-
-        def weight_tiles(name, tag, codes_tag):
-            grouped = keep.tile([P, PACK * K], BF16, name=name + "_grouped", tag=tag, align_bytes=64)
-            codes = keep.tile([P, K], U32, name=name + "_codes", tag=codes_tag, align_bytes=64)
-            scales = keep.tile([P, K], U8, name=name + "_scales", align_bytes=64)
-            return grouped, codes, scales
-
-        def cast_views(raw, grouped):
-            src = raw[:].rearrange("p (j q t i) -> p t q j i", j=PACK, t=PACK, i=4)
-            dst = grouped[:].rearrange("p (t q i j) -> p t q j i", j=PACK, t=PACK, i=4)
+        def cast_views(raw, rounded):
+            src = raw[:].rearrange("p (j q t r) -> p t q j r", j=PACK, t=PACK, r=RUN)
+            dst = rounded[:].rearrange("p (t q r j) -> p t q j r", j=PACK, t=PACK, r=RUN)
             return src, dst
 
-        def quantize(grouped, codes, scales, c0, c1):
+        def quantize(rounded, codes, scales, c0, c1):
             nc.vector.quantize_mx(
                 out=codes[:, c0:c1].bitcast(FP8X4),
                 scales=scales[:, c0:c1],
-                in_=grouped[:, PACK * c0 : PACK * c1],
+                in_=rounded[:, PACK * c0 : PACK * c1],
             )
 
-        def tower_matmuls(w_codes, w_scales, codes, scales, row, c):
+        def tower_step(w_codes, w_scales, codes, scales, scale_row, hidden, c):
             cols = slice(c * CHUNK, (c + 1) * CHUNK)
             bank = tower_psum.tile([P, PACK, CHUNK], F32, name="tower_bank")
             for t in range(PACK):
-                wc = slice(t * P, (t + 1) * P)
+                w_cols = slice(t * P, (t + 1) * P)
                 nc.tensor.matmul_mx(
                     out=bank[:, t, :],
-                    lhsT=w_codes[:, wc].bitcast(FP8X4),
-                    lhsT_scale=w_scales[:, wc],
+                    lhsT=w_codes[:, w_cols].bitcast(FP8X4),
+                    lhsT_scale=w_scales[:, w_cols],
                     rhs=codes[:, cols].bitcast(FP8X4),
-                    rhs_scale=scales[row:P, cols],
+                    rhs_scale=scales[scale_row:P, cols],
                     start=True,
                     stop=True,
                 )
-            return bank
-
-        def gelu(bank, hidden, c):
             dst = hidden[:, PACK * c * CHUNK : PACK * (c + 1) * CHUNK].rearrange("p (n t) -> p n t", t=PACK)
             nc.scalar.activation(dst, bank[:].rearrange("p t n -> p n t"), GELU)
 
-        nc.vector.tensor_copy(e_codes[:], e_tab[:].indirect(cand_sb[:]))
-        nc.vector.tensor_copy(e_sc[:], es_tab[:].indirect(cand_sb[:]))
+        e_codes = mx_tile([P, PICKED], U32, "e_codes", "e_codes")
+        e_picked_scales = mx_tile([P, PICKED], U8, "e_picked_scales", "e_picked_scales")
+        nc.vector.tensor_copy(e_codes[:], e_table[:].indirect(cand_sb[:]))
+        nc.vector.tensor_copy(e_picked_scales[:], e_scale_table[:].indirect(cand_sb[:]))
 
-        w2_grouped = keep.tile([P, PACK * K], BF16, name="w2_grouped", tag="stage", align_bytes=64)
-        src, dst = cast_views(w2_raw, w2_grouped)
+        w2_rounded = mx_tile([P, PACK * HIDDEN], BF16, "w2_rounded", "rounded_then_x_codes")
+        src, dst = cast_views(w2_raw, w2_rounded)
         nc.vector.tensor_copy(dst[:, 0], src[:, 0])
         for t in range(1, PACK):
             nc.scalar.copy(dst[:, t], src[:, t])
-        x_sc = keep.tile([P, PICKED], U8, name="x_sc", align_bytes=64)
-        nc.vector.tensor_copy(x_sc[:], xs_tab[:].indirect(offs_sb[:]))
-        w2_codes = keep.tile([P, K], U32, name="w2_codes", tag="xs_slot", align_bytes=64)
-        w2_scales = keep.tile([P, K], U8, name="w2_scales", align_bytes=64)
+        x_picked_scales = mx_tile([P, PICKED], U8, "x_picked_scales", "x_picked_scales")
+        nc.vector.tensor_copy(x_picked_scales[:], x_scale_table[:].indirect(offs_sb[:]))
+        w2_codes = mx_tile([P, HIDDEN], U32, "w2_codes", "x_scale_table_then_w2_codes")
+        w2_scales = mx_tile([P, HIDDEN], U8, "w2_scales", "w2_scales")
         for t in range(PACK):
-            quantize(w2_grouped, w2_codes, w2_scales, t * P, (t + 1) * P)
+            quantize(w2_rounded, w2_codes, w2_scales, t * P, (t + 1) * P)
 
-        d_hidden = keep.tile([P, PACK * K], BF16, name="d_hidden", align_bytes=64)
+        d_rounded = mx_tile([P, PACK * PICKED], BF16, "d_rounded", "d_rounded")
         for c in range(CHUNKS):
-            bank = tower_matmuls(w2_codes, w2_scales, e_codes, e_sc, E_ROW, c)
-            gelu(bank, d_hidden, c)
+            tower_step(w2_codes, w2_scales, e_codes, e_picked_scales, ITEM_SCALE_ROW, d_rounded, c)
 
-        w1_grouped, w1_codes, w1_scales = weight_tiles("w1", "stage", "w1_codes")
-        src, dst = cast_views(w1_raw, w1_grouped)
-        nc.vector.tensor_copy(dst[:, 0:2], src[:, 0:2])
-        nc.vector.tensor_copy(dst[:, 2:4], src[:, 2:4])
-        quantize(w1_grouped, w1_codes, w1_scales, 0, 256)
-        quantize(w1_grouped, w1_codes, w1_scales, 256, 512)
+        w1_rounded = mx_tile([P, PACK * HIDDEN], BF16, "w1_rounded", "rounded_then_x_codes")
+        w1_codes = mx_tile([P, HIDDEN], U32, "w1_codes", "w1_codes")
+        w1_scales = mx_tile([P, HIDDEN], U8, "w1_scales", "w1_scales")
+        src, dst = cast_views(w1_raw, w1_rounded)
+        for h in range(2):
+            nc.vector.tensor_copy(dst[:, 2 * h : 2 * h + 2], src[:, 2 * h : 2 * h + 2])
+        for h in range(2):
+            quantize(w1_rounded, w1_codes, w1_scales, h * HIDDEN // 2, (h + 1) * HIDDEN // 2)
 
-        x_codes = keep.tile([P, PICKED], U32, name="x_codes", tag="stage", align_bytes=64)
-        for g in range(PICKED // X_PIECE):
+        x_codes = mx_tile([P, PICKED], U32, "x_codes", "rounded_then_x_codes")
+        for h in range(2):
             nc.vector.tensor_copy(
-                x_codes[:, g * X_PIECE : (g + 1) * X_PIECE],
-                x_tab[:].indirect(offs_sb[:, g * X_PIECE // 16 : (g + 1) * X_PIECE // 16]),
+                x_codes[:, h * HALF : (h + 1) * HALF],
+                x_table[:].indirect(offs_sb[:, h * HALF // LIST_ROWS : (h + 1) * HALF // LIST_ROWS]),
             )
-        d_codes = keep.tile([P, K], U32, name="d_codes", tag="x_slot", align_bytes=64)
-        d_scales = keep.tile([P, K], U8, name="d_scales", align_bytes=64)
-        quantize(d_hidden, d_codes, d_scales, 0, 256)
-        quantize(d_hidden, d_codes, d_scales, 256, 512)
 
-        p_hidden, p_codes, p_scales = weight_tiles("p", "p_hidden", "p_codes")
+        d_codes = mx_tile([P, PICKED], U32, "d_codes", "x_table_then_d_codes")
+        d_scales = mx_tile([P, PICKED], U8, "d_scales", "d_scales")
+        for h in range(2):
+            quantize(d_rounded, d_codes, d_scales, h * HALF, (h + 1) * HALF)
+
+        p_rounded = mx_tile([P, PACK * PICKED], BF16, "p_rounded", "p_rounded")
+        p_codes = mx_tile([P, PICKED], U32, "p_codes", "p_codes")
+        p_scales = mx_tile([P, PICKED], U8, "p_scales", "p_scales")
         scores = [score_psum.tile([P, PICKED], F32, name="score%d" % c) for c in range(CHUNKS)]
 
-        def score_pass(c, l_codes, l_scales, r_codes, r_scales, first):
+        def user_tower(c):
+            tower_step(w1_codes, w1_scales, x_codes, x_picked_scales, 0, p_rounded, c)
+            quantize(p_rounded, p_codes, p_scales, c * CHUNK, (c + 1) * CHUNK)
+
+        def score_pass(c, user_codes, user_scales, item_codes, item_scales, first):
             cols = slice(c * CHUNK, (c + 1) * CHUNK)
             nc.tensor.matmul_mx(
                 out=scores[c][:],
-                lhsT=l_codes[:, cols].bitcast(FP8X4),
-                lhsT_scale=l_scales[:, cols],
-                rhs=r_codes[:].bitcast(FP8X4),
-                rhs_scale=r_scales,
+                lhsT=user_codes[:, cols].bitcast(FP8X4),
+                lhsT_scale=user_scales[:, cols],
+                rhs=item_codes[:].bitcast(FP8X4),
+                rhs_scale=item_scales,
                 start=first,
                 stop=not first,
             )
 
-        def user_tower(c):
-            bank = tower_matmuls(w1_codes, w1_scales, x_codes, x_sc, 0, c)
-            gelu(bank, p_hidden, c)
-            quantize(p_hidden, p_codes, p_scales, c * CHUNK, (c + 1) * CHUNK)
-
-        def finish(c, pieces):
-            score_pass(c, x_codes, x_sc, e_codes, e_sc[E_ROW:P, :], True)
+        def finish(c):
+            score_pass(c, x_codes, x_picked_scales, e_codes, e_picked_scales[ITEM_SCALE_ROW:P, :], True)
             score_pass(c, p_codes, p_scales, d_codes, d_scales[:], False)
-            width = PICKED // pieces
-            for h in range(pieces):
-                cols = slice(h * width, (h + 1) * width)
-                half = keep.tile([P, width], F32, name="half%d_%d" % (c, h))
-                res = keep.tile([P, width], F32, name="res%d_%d" % (c, h))
-                nc.scalar.activation(half[:], scores[c][:, cols], TANH, scale=0.5)
-                nc.vector.tensor_scalar(res[:], half[:], 0.5, 0.5, MULT, ADD)
-                nc.sync.dma_start(out[c * CHUNK : (c + 1) * CHUNK, cols], res[:])
+            for h in range(2):
+                cols = slice(h * HALF, (h + 1) * HALF)
+                tanh_half = keep.tile([P, HALF], F32, name="tanh_%d_%d" % (c, h))
+                result = keep.tile([P, HALF], F32, name="result_%d_%d" % (c, h))
+                nc.scalar.activation(tanh_half[:], scores[c][:, cols], TANH, bias=zero_bias[:], scale=0.5)
+                nc.vector.tensor_scalar(result[:], tanh_half[:], 0.5, 0.5, MULT, ADD)
+                nc.sync.dma_start(out[c * CHUNK : (c + 1) * CHUNK, cols], result[:])
 
-        user_tower(0)
-        user_tower(1)
-        user_tower(2)
-        finish(0, 1)
-        user_tower(3)
-        finish(1, 1)
-        finish(2, 1)
-        finish(3, 2)
+        for c in range(CHUNKS - 1):
+            user_tower(c)
+        finish(0)
+        user_tower(CHUNKS - 1)
+        for c in range(1, CHUNKS):
+            finish(c)

@@ -10,6 +10,7 @@ U16 = mybir.dt.uint16
 U8 = mybir.dt.uint8
 FP8X4 = mybir.dt.float8_e4m3fn_x4
 GELU = mybir.ActivationFunctionType.Gelu_apprx_tanh
+IDENTITY = mybir.ActivationFunctionType.Identity
 TANH = mybir.ActivationFunctionType.Tanh
 MULT = mybir.AluOpType.mult
 ADD = mybir.AluOpType.add
@@ -51,7 +52,7 @@ def tile_picked_zneumf_gelu_p_kernel(
         x_scale_table = mx_tile([P, USERS], U8, "x_scale_table", "x_scale_table_then_w2_codes")
         e_scale_table = mx_tile([P, ITEMS], U8, "e_scale_table", "e_scale_table")
         w2_raw = mx_tile([P, PACK * HIDDEN], F32, "w2_raw", "w2_raw")
-        zero_in = keep.tile([P, 1], F32, name="zero_in")
+        zero_in = mx_tile([P, 1], F32, "zero_in", "zero_in_then_d_rounded")
         zero_bias = keep.tile([P, 1], F32, name="zero_bias")
 
         nc.vector.memset(e_scale_table[:].bitcast(I32), 0)
@@ -86,7 +87,7 @@ def tile_picked_zneumf_gelu_p_kernel(
 
         def cast_views(raw, rounded):
             src = raw[:].rearrange("p (j q t r) -> p t q j r", j=PACK, t=PACK, r=RUN)
-            dst = rounded[:].rearrange("p (t q r j) -> p t q j r", j=PACK, t=PACK, r=RUN)
+            dst = rounded[:].rearrange("p (t q r j) -> p t q j r", j=PACK, q=P // RUN, r=RUN)
             return src, dst
 
         def quantize(rounded, codes, scales, c0, c1):
@@ -118,6 +119,18 @@ def tile_picked_zneumf_gelu_p_kernel(
         nc.vector.tensor_copy(e_codes[:], e_table[:].indirect(cand_sb[:]))
         nc.vector.tensor_copy(e_picked_scales[:], e_scale_table[:].indirect(cand_sb[:]))
 
+        scores = [score_psum.tile([P, PICKED], F32, name="score%d" % c) for c in range(CHUNKS)]
+        for c in range(4):
+            nc.tensor.matmul_mx(
+                out=scores[c][:],
+                lhsT=e_codes[:, :P].bitcast(FP8X4),
+                lhsT_scale=e_picked_scales[ITEM_SCALE_ROW:P, :P],
+                rhs=e_codes[:].bitcast(FP8X4),
+                rhs_scale=e_picked_scales[ITEM_SCALE_ROW:P, :],
+                start=True,
+                stop=True,
+            )
+
         w2_rounded = mx_tile([P, PACK * HIDDEN], BF16, "w2_rounded", "rounded_then_x_codes")
         src, dst = cast_views(w2_raw, w2_rounded)
         nc.vector.tensor_copy(dst[:, 0], src[:, 0])
@@ -130,18 +143,25 @@ def tile_picked_zneumf_gelu_p_kernel(
         for t in range(PACK):
             quantize(w2_rounded, w2_codes, w2_scales, t * P, (t + 1) * P)
 
-        d_rounded = mx_tile([P, PACK * PICKED], BF16, "d_rounded", "d_rounded")
+        w1_last = mx_tile([P, PACK * P], BF16, "w1_last", "w1_last")
+        src, dst = cast_views(w1_raw, w1_last)
+        nc.scalar.activation(dst[:, 0], src[:, PACK - 1], IDENTITY, bias=zero_in[:])
+
+        d_rounded = mx_tile([P, PACK * PICKED], BF16, "d_rounded", "zero_in_then_d_rounded")
         for c in range(CHUNKS):
             tower_step(w2_codes, w2_scales, e_codes, e_picked_scales, ITEM_SCALE_ROW, d_rounded, c)
 
-        w1_rounded = mx_tile([P, PACK * HIDDEN], BF16, "w1_rounded", "rounded_then_x_codes")
+        w1_rounded = mx_tile([P, (PACK - 1) * HIDDEN], BF16, "w1_rounded", "rounded_then_x_codes")
         w1_codes = mx_tile([P, HIDDEN], U32, "w1_codes", "w1_codes")
         w1_scales = mx_tile([P, HIDDEN], U8, "w1_scales", "w1_scales")
         src, dst = cast_views(w1_raw, w1_rounded)
-        for h in range(2):
-            nc.vector.tensor_copy(dst[:, 2 * h : 2 * h + 2], src[:, 2 * h : 2 * h + 2])
-        for h in range(2):
-            quantize(w1_rounded, w1_codes, w1_scales, h * HIDDEN // 2, (h + 1) * HIDDEN // 2)
+        nc.vector.tensor_copy(dst[:, 0:2], src[:, 0:2])
+        nc.vector.tensor_copy(dst[:, 2], src[:, 2])
+        nc.vector.quantize_mx(
+            out=w1_codes[:, 3 * P :].bitcast(FP8X4), scales=w1_scales[:, 3 * P :], in_=w1_last[:]
+        )
+        quantize(w1_rounded, w1_codes, w1_scales, 0, 2 * P)
+        quantize(w1_rounded, w1_codes, w1_scales, 2 * P, 3 * P)
 
         x_codes = mx_tile([P, PICKED], U32, "x_codes", "rounded_then_x_codes")
         for h in range(2):
@@ -158,7 +178,6 @@ def tile_picked_zneumf_gelu_p_kernel(
         p_rounded = mx_tile([P, PACK * PICKED], BF16, "p_rounded", "p_rounded")
         p_codes = mx_tile([P, PICKED], U32, "p_codes", "p_codes")
         p_scales = mx_tile([P, PICKED], U8, "p_scales", "p_scales")
-        scores = [score_psum.tile([P, PICKED], F32, name="score%d" % c) for c in range(CHUNKS)]
 
         def user_tower(c):
             tower_step(w1_codes, w1_scales, x_codes, x_picked_scales, 0, p_rounded, c)

@@ -40,8 +40,7 @@ def tile_picked_zneumf_gelu_p_kernel(
     nc = tc.nc
     with ExitStack() as ctx:
         keep = ctx.enter_context(tc.tile_pool(name="keep", bufs=1))
-        tower_psum = ctx.enter_context(tc.psum_pool(name="tower_psum", bufs=CHUNKS))
-        score_psum = ctx.enter_context(tc.psum_pool(name="score_psum", bufs=1))
+        psum = ctx.enter_context(tc.psum_pool(name="psum", bufs=1))
 
         def mx_tile(shape, dtype, name, tag):
             return keep.tile(shape, dtype, name=name, tag=tag, align_bytes=64)
@@ -56,9 +55,9 @@ def tile_picked_zneumf_gelu_p_kernel(
         zero_bias = keep.tile([P, 1], F32, name="zero_bias")
 
         nc.vector.memset(e_scale_table[:].bitcast(I32), 0)
-        nc.gpsimd.memset(x_scale_table[:].bitcast(I32), 0)
         nc.vector.memset(zero_in[:], 0.0)
         nc.scalar.activation(zero_bias[:], zero_in[:], GELU)
+        nc.vector.memset(x_scale_table[:].bitcast(I32), 0)
 
         def load_words(table, words):
             nc.sync.dma_start(table[:].bitcast(I32), words[0].rearrange("p n j -> p (n j)").bitcast(I32))
@@ -76,9 +75,9 @@ def tile_picked_zneumf_gelu_p_kernel(
 
         load_words(e_table, e_words)
         nc.sync.dma_start(cand_sb[:], cand)
-        nc.sync.dma_start(offs_sb[:], offs)
         load_scale_rows(e_scale_table, e_scales, ITEM_SCALE_ROW)
         load_weight(w2_raw, w2)
+        nc.sync.dma_start(offs_sb[:], offs)
         load_scale_rows(x_scale_table, x_scales, 0)
         w1_raw = mx_tile([P, PACK * HIDDEN], F32, "w1_raw", "w1_raw")
         x_table = mx_tile([P, USERS], U32, "x_table", "x_table_then_d_codes")
@@ -97,9 +96,9 @@ def tile_picked_zneumf_gelu_p_kernel(
                 in_=rounded[:, PACK * c0 : PACK * c1],
             )
 
-        def tower_step(w_codes, w_scales, codes, scales, scale_row, hidden, c):
+        def tower_step(w_codes, w_scales, codes, scales, scale_row, hidden, c, bank_tag):
             cols = slice(c * CHUNK, (c + 1) * CHUNK)
-            bank = tower_psum.tile([P, PACK, CHUNK], F32, name="tower_bank")
+            bank = psum.tile([P, PACK, CHUNK], F32, name="tower_bank", tag=bank_tag)
             for t in range(PACK):
                 w_cols = slice(t * P, (t + 1) * P)
                 nc.tensor.matmul_mx(
@@ -111,25 +110,16 @@ def tile_picked_zneumf_gelu_p_kernel(
                     start=True,
                     stop=True,
                 )
-            dst = hidden[:, PACK * c * CHUNK : PACK * (c + 1) * CHUNK].rearrange("p (n t) -> p n t", t=PACK)
-            nc.scalar.activation(dst, bank[:].rearrange("p t n -> p n t"), GELU)
+            return bank
+
+        def gelu(bank, hidden, c, n0, n1):
+            dst = hidden[:, PACK * (c * CHUNK + n0) : PACK * (c * CHUNK + n1)].rearrange("p (n t) -> p n t", t=PACK)
+            nc.scalar.activation(dst, bank[:, :, n0:n1].rearrange("p t n -> p n t"), GELU)
 
         e_codes = mx_tile([P, PICKED], U32, "e_codes", "e_codes")
         e_picked_scales = mx_tile([P, PICKED], U8, "e_picked_scales", "e_picked_scales")
         nc.vector.tensor_copy(e_codes[:], e_table[:].indirect(cand_sb[:]))
         nc.vector.tensor_copy(e_picked_scales[:], e_scale_table[:].indirect(cand_sb[:]))
-
-        scores = [score_psum.tile([P, PICKED], F32, name="score%d" % c) for c in range(CHUNKS)]
-        for c in range(4):
-            nc.tensor.matmul_mx(
-                out=scores[c][:],
-                lhsT=e_codes[:, :P].bitcast(FP8X4),
-                lhsT_scale=e_picked_scales[ITEM_SCALE_ROW:P, :P],
-                rhs=e_codes[:].bitcast(FP8X4),
-                rhs_scale=e_picked_scales[ITEM_SCALE_ROW:P, :],
-                start=True,
-                stop=True,
-            )
 
         w2_rounded = mx_tile([P, PACK * HIDDEN], BF16, "w2_rounded", "rounded_then_x_codes")
         src, dst = cast_views(w2_raw, w2_rounded)
@@ -140,8 +130,7 @@ def tile_picked_zneumf_gelu_p_kernel(
         nc.vector.tensor_copy(x_picked_scales[:], x_scale_table[:].indirect(offs_sb[:]))
         w2_codes = mx_tile([P, HIDDEN], U32, "w2_codes", "x_scale_table_then_w2_codes")
         w2_scales = mx_tile([P, HIDDEN], U8, "w2_scales", "w2_scales")
-        for t in range(PACK):
-            quantize(w2_rounded, w2_codes, w2_scales, t * P, (t + 1) * P)
+        quantize(w2_rounded, w2_codes, w2_scales, 0, HIDDEN)
 
         w1_last = mx_tile([P, PACK * P], BF16, "w1_last", "w1_last")
         src, dst = cast_views(w1_raw, w1_last)
@@ -149,7 +138,7 @@ def tile_picked_zneumf_gelu_p_kernel(
 
         d_rounded = mx_tile([P, PACK * PICKED], BF16, "d_rounded", "zero_in_then_d_rounded")
         for c in range(CHUNKS):
-            tower_step(w2_codes, w2_scales, e_codes, e_picked_scales, ITEM_SCALE_ROW, d_rounded, c)
+            gelu(tower_step(w2_codes, w2_scales, e_codes, e_picked_scales, ITEM_SCALE_ROW, d_rounded, c, "bank%d" % c), d_rounded, c, 0, CHUNK)
 
         w1_rounded = mx_tile([P, (PACK - 1) * HIDDEN], BF16, "w1_rounded", "rounded_then_x_codes")
         w1_codes = mx_tile([P, HIDDEN], U32, "w1_codes", "w1_codes")
@@ -178,9 +167,12 @@ def tile_picked_zneumf_gelu_p_kernel(
         p_rounded = mx_tile([P, PACK * PICKED], BF16, "p_rounded", "p_rounded")
         p_codes = mx_tile([P, PICKED], U32, "p_codes", "p_codes")
         p_scales = mx_tile([P, PICKED], U8, "p_scales", "p_scales")
+        scores = {}
 
         def user_tower(c):
-            tower_step(w1_codes, w1_scales, x_codes, x_picked_scales, 0, p_rounded, c)
+            return tower_step(w1_codes, w1_scales, x_codes, x_picked_scales, 0, p_rounded, c, "bank%d" % ((CHUNKS + 1 + c) % (2 * CHUNKS)))
+
+        def quantize_p(c):
             quantize(p_rounded, p_codes, p_scales, c * CHUNK, (c + 1) * CHUNK)
 
         def score_pass(c, user_codes, user_scales, item_codes, item_scales, first):
@@ -196,19 +188,30 @@ def tile_picked_zneumf_gelu_p_kernel(
             )
 
         def finish(c):
+            scores[c] = psum.tile([P, PICKED], F32, name="score%d" % c, tag="bank%d" % (CHUNKS + c))
             score_pass(c, x_codes, x_picked_scales, e_codes, e_picked_scales[ITEM_SCALE_ROW:P, :], True)
             score_pass(c, p_codes, p_scales, d_codes, d_scales[:], False)
-            for h in range(2):
-                cols = slice(h * HALF, (h + 1) * HALF)
-                tanh_half = keep.tile([P, HALF], F32, name="tanh_%d_%d" % (c, h))
-                result = keep.tile([P, HALF], F32, name="result_%d_%d" % (c, h))
-                nc.scalar.activation(tanh_half[:], scores[c][:, cols], TANH, bias=zero_bias[:], scale=0.5)
-                nc.vector.tensor_scalar(result[:], tanh_half[:], 0.5, 0.5, MULT, ADD)
-                nc.sync.dma_start(out[c * CHUNK : (c + 1) * CHUNK, cols], result[:])
 
-        for c in range(CHUNKS - 1):
-            user_tower(c)
+        def leave(c, h):
+            cols = slice(h * HALF, (h + 1) * HALF)
+            tanh_half = keep.tile([P, HALF], F32, name="tanh_%d_%d" % (c, h))
+            result = keep.tile([P, HALF], F32, name="result_%d_%d" % (c, h))
+            nc.scalar.activation(tanh_half[:], scores[c][:, cols], TANH, bias=zero_bias[:], scale=0.5)
+            nc.vector.tensor_scalar(result[:], tanh_half[:], 0.5, 0.5, MULT, ADD)
+            nc.sync.dma_start(out[c * CHUNK : (c + 1) * CHUNK, cols], result[:])
+
+        last = CHUNKS - 1
+        for c in range(last):
+            gelu(user_tower(c), p_rounded, c, 0, CHUNK)
+            quantize_p(c)
+        bank = user_tower(last)
+        gelu(bank, p_rounded, last, 0, CHUNK // 2)
         finish(0)
-        user_tower(CHUNKS - 1)
+        leave(0, 0)
+        gelu(bank, p_rounded, last, CHUNK // 2, CHUNK)
+        quantize_p(last)
+        leave(0, 1)
         for c in range(1, CHUNKS):
             finish(c)
+            leave(c, 0)
+            leave(c, 1)

@@ -20,6 +20,7 @@ PACK = 4
 RUN = 4
 QUADRANT = 32
 SCALE_ROWS = 16
+SPREAD = P // SCALE_ROWS
 LIST_ROWS = 16
 K = 512
 HIDDEN = 512
@@ -50,7 +51,7 @@ def tile_picked_zneumf_gelu_p_kernel(
         e_table = mx_tile([P, ITEMS], U32, "e_table", "e_table")
         x_scale_table = mx_tile([P, USERS], U8, "x_scale_table", "x_scale_table_then_w2_codes")
         e_scale_table = mx_tile([P, ITEMS], U8, "e_scale_table", "e_scale_table")
-        w2_raw = mx_tile([P, PACK * HIDDEN], F32, "w2_raw", "w2_raw")
+        w2_raw = mx_tile([P, PACK * HIDDEN], F32, "w2_raw", "w2_raw_then_x_scale_rows")
         zero_in = mx_tile([P, 1], F32, "zero_in", "zero_in_then_d_rounded")
         zero_bias = keep.tile([P, 1], F32, name="zero_bias")
 
@@ -78,7 +79,7 @@ def tile_picked_zneumf_gelu_p_kernel(
         load_scale_rows(e_scale_table, e_scales, ITEM_SCALE_ROW)
         load_weight(w2_raw, w2)
         nc.sync.dma_start(offs_sb[:], offs)
-        load_scale_rows(x_scale_table, x_scales, 0)
+        nc.sync.dma_start(x_scale_table[0:P:SPREAD, :].bitcast(I32), x_scales[0].bitcast(I32))
         w1_raw = mx_tile([P, PACK * HIDDEN], F32, "w1_raw", "w1_raw")
         x_table = mx_tile([P, USERS], U32, "x_table", "x_table_then_d_codes")
         load_weight(w1_raw, w1)
@@ -128,6 +129,13 @@ def tile_picked_zneumf_gelu_p_kernel(
             nc.scalar.copy(dst[:, t], src[:, t])
         x_picked_scales = mx_tile([P, PICKED], U8, "x_picked_scales", "x_picked_scales")
         nc.vector.tensor_copy(x_picked_scales[:], x_scale_table[:].indirect(offs_sb[:]))
+        x_scale_rows = mx_tile([P, PICKED], U8, "x_scale_rows", "w2_raw_then_x_scale_rows")
+        nc.vector.tensor_copy(x_scale_rows[:].bitcast(I32), x_picked_scales[:].bitcast(I32))
+        for r in range(1, 4):
+            nc.scalar.dma_start(
+                x_scale_rows[r:P:QUADRANT, :].bitcast(I32),
+                x_picked_scales[SPREAD * r : P : QUADRANT, :].bitcast(I32),
+            )
         w2_codes = mx_tile([P, HIDDEN], U32, "w2_codes", "x_scale_table_then_w2_codes")
         w2_scales = mx_tile([P, HIDDEN], U8, "w2_scales", "w2_scales")
         quantize(w2_rounded, w2_codes, w2_scales, 0, HIDDEN)
@@ -170,7 +178,7 @@ def tile_picked_zneumf_gelu_p_kernel(
         scores = {}
 
         def user_tower(c):
-            return tower_step(w1_codes, w1_scales, x_codes, x_picked_scales, 0, p_rounded, c, "bank%d" % ((CHUNKS + 1 + c) % (2 * CHUNKS)))
+            return tower_step(w1_codes, w1_scales, x_codes, x_scale_rows, 0, p_rounded, c, "bank%d" % ((CHUNKS + 1 + c) % (2 * CHUNKS)))
 
         def quantize_p(c):
             quantize(p_rounded, p_codes, p_scales, c * CHUNK, (c + 1) * CHUNK)
@@ -189,7 +197,7 @@ def tile_picked_zneumf_gelu_p_kernel(
 
         def finish(c):
             scores[c] = psum.tile([P, PICKED], F32, name="score%d" % c, tag="bank%d" % (CHUNKS + c))
-            score_pass(c, x_codes, x_picked_scales, e_codes, e_picked_scales[ITEM_SCALE_ROW:P, :], True)
+            score_pass(c, x_codes, x_scale_rows, e_codes, e_picked_scales[ITEM_SCALE_ROW:P, :], True)
             score_pass(c, p_codes, p_scales, d_codes, d_scales[:], False)
 
         def leave(c, h):

@@ -20,6 +20,7 @@ PACK = 4
 RUN = 4
 QUADRANT = 32
 SCALE_ROWS = 16
+QUADRANT_ROWS = SCALE_ROWS * QUADRANT // P
 SPREAD = P // SCALE_ROWS
 LIST_ROWS = 16
 K = 512
@@ -30,6 +31,7 @@ PICKED = 512
 CHUNK = 128
 CHUNKS = PICKED // CHUNK
 HALF = PICKED // 2
+BANKS = 8
 ITEM_SCALE_ROW = 4
 
 FLOPS = 2 * PICKED * (2 * K * HIDDEN + HIDDEN * PICKED + K * PICKED)
@@ -46,14 +48,17 @@ def tile_picked_zneumf_gelu_p_kernel(
         def mx_tile(shape, dtype, name, tag):
             return keep.tile(shape, dtype, name=name, tag=tag, align_bytes=64)
 
+        def psum_bank(shape, name, bank):
+            return psum.tile(shape, F32, name=name, tag="bank%d" % bank)
+
         offs_sb = keep.tile([P, PICKED // LIST_ROWS], U16, name="offs_sb")
         cand_sb = keep.tile([P, PICKED // LIST_ROWS], U16, name="cand_sb")
         e_table = mx_tile([P, ITEMS], U32, "e_table", "e_table")
         x_scale_table = mx_tile([P, USERS], U8, "x_scale_table", "x_scale_table_then_w2_codes")
         e_scale_table = mx_tile([P, ITEMS], U8, "e_scale_table", "e_scale_table")
         w2_raw = mx_tile([P, PACK * HIDDEN], F32, "w2_raw", "w2_raw_then_x_scale_rows")
-        zero_in = mx_tile([P, 1], F32, "zero_in", "zero_in_then_d_rounded")
-        zero_bias = keep.tile([P, 1], F32, name="zero_bias")
+        zero_in = keep.tile([P, 1], F32, name="zero_in")
+        zero_bias = mx_tile([P, 1], F32, "zero_bias", "zero_bias_then_d_rounded")
 
         nc.vector.memset(e_scale_table[:].bitcast(I32), 0)
         nc.vector.memset(zero_in[:], 0.0)
@@ -63,20 +68,16 @@ def tile_picked_zneumf_gelu_p_kernel(
         def load_words(table, words):
             nc.sync.dma_start(table[:].bitcast(I32), words[0].rearrange("p n j -> p (n j)").bitcast(I32))
 
-        def load_scale_rows(table, scales, first_row):
-            rows_per_quadrant = SCALE_ROWS * QUADRANT // P
-            for r in range(rows_per_quadrant):
-                nc.sync.dma_start(
-                    table[first_row + r : P : QUADRANT, :].bitcast(I32),
-                    scales[0][r:SCALE_ROWS:rows_per_quadrant, :].bitcast(I32),
-                )
-
         def load_weight(raw, w):
             nc.sync.dma_start(raw[:], w.rearrange("(p j) c -> p (j c)", j=PACK))
 
         load_words(e_table, e_words)
         nc.sync.dma_start(cand_sb[:], cand)
-        load_scale_rows(e_scale_table, e_scales, ITEM_SCALE_ROW)
+        for r in range(QUADRANT_ROWS):
+            nc.sync.dma_start(
+                e_scale_table[ITEM_SCALE_ROW + r : P : QUADRANT, :].bitcast(I32),
+                e_scales[0][r:SCALE_ROWS:QUADRANT_ROWS, :].bitcast(I32),
+            )
         load_weight(w2_raw, w2)
         nc.sync.dma_start(offs_sb[:], offs)
         nc.sync.dma_start(x_scale_table[0:P:SPREAD, :].bitcast(I32), x_scales[0].bitcast(I32))
@@ -85,80 +86,82 @@ def tile_picked_zneumf_gelu_p_kernel(
         load_weight(w1_raw, w1)
         load_words(x_table, x_words)
 
-        def cast_views(raw, rounded):
+        def rounding_views(raw, rounded):
             src = raw[:].rearrange("p (j q t r) -> p t q j r", j=PACK, t=PACK, r=RUN)
             dst = rounded[:].rearrange("p (t q r j) -> p t q j r", j=PACK, q=P // RUN, r=RUN)
             return src, dst
 
-        def quantize(rounded, codes, scales, c0, c1):
+        def quantize(rounded, codes, scales, c0, c1, rounded_from=0):
             nc.vector.quantize_mx(
                 out=codes[:, c0:c1].bitcast(FP8X4),
                 scales=scales[:, c0:c1],
-                in_=rounded[:, PACK * c0 : PACK * c1],
+                in_=rounded[:, PACK * (c0 - rounded_from) : PACK * (c1 - rounded_from)],
             )
 
-        def tower_step(w_codes, w_scales, codes, scales, scale_row, hidden, c, bank_tag):
+        def tower_products(w_codes, w_scales, codes, scales, c, bank):
             cols = slice(c * CHUNK, (c + 1) * CHUNK)
-            bank = psum.tile([P, PACK, CHUNK], F32, name="tower_bank", tag=bank_tag)
+            products = psum_bank([P, PACK, CHUNK], "products", bank)
             for t in range(PACK):
-                w_cols = slice(t * P, (t + 1) * P)
+                quarter = slice(t * P, (t + 1) * P)
                 nc.tensor.matmul_mx(
-                    out=bank[:, t, :],
-                    lhsT=w_codes[:, w_cols].bitcast(FP8X4),
-                    lhsT_scale=w_scales[:, w_cols],
+                    out=products[:, t, :],
+                    lhsT=w_codes[:, quarter].bitcast(FP8X4),
+                    lhsT_scale=w_scales[:, quarter],
                     rhs=codes[:, cols].bitcast(FP8X4),
-                    rhs_scale=scales[scale_row:P, cols],
+                    rhs_scale=scales[:, cols],
                     start=True,
                     stop=True,
                 )
-            return bank
+            return products
 
-        def gelu(bank, hidden, c, n0, n1):
-            dst = hidden[:, PACK * (c * CHUNK + n0) : PACK * (c * CHUNK + n1)].rearrange("p (n t) -> p n t", t=PACK)
-            nc.scalar.activation(dst, bank[:, :, n0:n1].rearrange("p t n -> p n t"), GELU)
+        def gelu(products, rounded, c, n0=0, n1=CHUNK):
+            dst = rounded[:, PACK * (c * CHUNK + n0) : PACK * (c * CHUNK + n1)].rearrange("p (n t) -> p n t", t=PACK)
+            nc.scalar.activation(dst, products[:, :, n0:n1].rearrange("p t n -> p n t"), GELU)
 
         e_codes = mx_tile([P, PICKED], U32, "e_codes", "e_codes")
-        e_picked_scales = mx_tile([P, PICKED], U8, "e_picked_scales", "e_picked_scales")
+        e_scale_rows = mx_tile([P, PICKED], U8, "e_scale_rows", "e_scale_rows")
         nc.vector.tensor_copy(e_codes[:], e_table[:].indirect(cand_sb[:]))
-        nc.vector.tensor_copy(e_picked_scales[:], e_scale_table[:].indirect(cand_sb[:]))
+        nc.vector.tensor_copy(e_scale_rows[:], e_scale_table[:].indirect(cand_sb[:]))
+        e_plane = e_scale_rows[ITEM_SCALE_ROW:P, :]
 
         w2_rounded = mx_tile([P, PACK * HIDDEN], BF16, "w2_rounded", "rounded_then_x_codes")
-        src, dst = cast_views(w2_raw, w2_rounded)
+        src, dst = rounding_views(w2_raw, w2_rounded)
         nc.vector.tensor_copy(dst[:, 0], src[:, 0])
         for t in range(1, PACK):
             nc.scalar.copy(dst[:, t], src[:, t])
-        x_picked_scales = mx_tile([P, PICKED], U8, "x_picked_scales", "x_picked_scales")
-        nc.vector.tensor_copy(x_picked_scales[:], x_scale_table[:].indirect(offs_sb[:]))
+        x_spread_scales = mx_tile([P, PICKED], U8, "x_spread_scales", "x_spread_scales")
+        nc.vector.tensor_copy(x_spread_scales[:], x_scale_table[:].indirect(offs_sb[:]))
+
         x_scale_rows = mx_tile([P, PICKED], U8, "x_scale_rows", "w2_raw_then_x_scale_rows")
-        nc.vector.tensor_copy(x_scale_rows[:].bitcast(I32), x_picked_scales[:].bitcast(I32))
-        for r in range(1, 4):
+        nc.vector.tensor_copy(x_scale_rows[:].bitcast(I32), x_spread_scales[:].bitcast(I32))
+        for r in range(1, QUADRANT_ROWS):
             nc.scalar.dma_start(
                 x_scale_rows[r:P:QUADRANT, :].bitcast(I32),
-                x_picked_scales[SPREAD * r : P : QUADRANT, :].bitcast(I32),
+                x_spread_scales[SPREAD * r : P : QUADRANT, :].bitcast(I32),
             )
+
         w2_codes = mx_tile([P, HIDDEN], U32, "w2_codes", "x_scale_table_then_w2_codes")
         w2_scales = mx_tile([P, HIDDEN], U8, "w2_scales", "w2_scales")
         quantize(w2_rounded, w2_codes, w2_scales, 0, HIDDEN)
 
-        w1_last = mx_tile([P, PACK * P], BF16, "w1_last", "w1_last")
-        src, dst = cast_views(w1_raw, w1_last)
-        nc.scalar.activation(dst[:, 0], src[:, PACK - 1], IDENTITY, bias=zero_in[:])
+        last_quarter = PACK - 1
+        w1_rounded_last = mx_tile([P, PACK * P], BF16, "w1_rounded_last", "w1_rounded_last")
+        src, dst = rounding_views(w1_raw, w1_rounded_last)
+        nc.scalar.activation(dst[:, 0], src[:, last_quarter], IDENTITY, bias=zero_bias[:])
 
-        d_rounded = mx_tile([P, PACK * PICKED], BF16, "d_rounded", "zero_in_then_d_rounded")
+        d_rounded = mx_tile([P, PACK * PICKED], BF16, "d_rounded", "zero_bias_then_d_rounded")
         for c in range(CHUNKS):
-            gelu(tower_step(w2_codes, w2_scales, e_codes, e_picked_scales, ITEM_SCALE_ROW, d_rounded, c, "bank%d" % c), d_rounded, c, 0, CHUNK)
+            gelu(tower_products(w2_codes, w2_scales, e_codes, e_plane, c, c), d_rounded, c)
 
-        w1_rounded = mx_tile([P, (PACK - 1) * HIDDEN], BF16, "w1_rounded", "rounded_then_x_codes")
+        w1_rounded = mx_tile([P, last_quarter * PACK * P], BF16, "w1_rounded", "rounded_then_x_codes")
         w1_codes = mx_tile([P, HIDDEN], U32, "w1_codes", "w1_codes")
         w1_scales = mx_tile([P, HIDDEN], U8, "w1_scales", "w1_scales")
-        src, dst = cast_views(w1_raw, w1_rounded)
+        src, dst = rounding_views(w1_raw, w1_rounded)
         nc.vector.tensor_copy(dst[:, 0:2], src[:, 0:2])
         nc.vector.tensor_copy(dst[:, 2], src[:, 2])
-        nc.vector.quantize_mx(
-            out=w1_codes[:, 3 * P :].bitcast(FP8X4), scales=w1_scales[:, 3 * P :], in_=w1_last[:]
-        )
+        quantize(w1_rounded_last, w1_codes, w1_scales, last_quarter * P, HIDDEN, last_quarter * P)
         quantize(w1_rounded, w1_codes, w1_scales, 0, 2 * P)
-        quantize(w1_rounded, w1_codes, w1_scales, 2 * P, 3 * P)
+        quantize(w1_rounded, w1_codes, w1_scales, 2 * P, last_quarter * P)
 
         x_codes = mx_tile([P, PICKED], U32, "x_codes", "rounded_then_x_codes")
         for h in range(2):
@@ -175,51 +178,47 @@ def tile_picked_zneumf_gelu_p_kernel(
         p_rounded = mx_tile([P, PACK * PICKED], BF16, "p_rounded", "p_rounded")
         p_codes = mx_tile([P, PICKED], U32, "p_codes", "p_codes")
         p_scales = mx_tile([P, PICKED], U8, "p_scales", "p_scales")
-        scores = {}
 
-        def user_tower(c):
-            return tower_step(w1_codes, w1_scales, x_codes, x_scale_rows, 0, p_rounded, c, "bank%d" % ((CHUNKS + 1 + c) % (2 * CHUNKS)))
+        def user_products(c):
+            return tower_products(w1_codes, w1_scales, x_codes, x_scale_rows[:], c, (CHUNKS + c + 1) % BANKS)
 
         def quantize_p(c):
             quantize(p_rounded, p_codes, p_scales, c * CHUNK, (c + 1) * CHUNK)
 
-        def score_pass(c, user_codes, user_scales, item_codes, item_scales, first):
-            cols = slice(c * CHUNK, (c + 1) * CHUNK)
-            nc.tensor.matmul_mx(
-                out=scores[c][:],
-                lhsT=user_codes[:, cols].bitcast(FP8X4),
-                lhsT_scale=user_scales[:, cols],
-                rhs=item_codes[:].bitcast(FP8X4),
-                rhs_scale=item_scales,
-                start=first,
-                stop=not first,
-            )
-
-        def finish(c):
-            scores[c] = psum.tile([P, PICKED], F32, name="score%d" % c, tag="bank%d" % (CHUNKS + c))
-            score_pass(c, x_codes, x_scale_rows, e_codes, e_picked_scales[ITEM_SCALE_ROW:P, :], True)
-            score_pass(c, p_codes, p_scales, d_codes, d_scales[:], False)
-
         def leave(c, h):
-            cols = slice(h * HALF, (h + 1) * HALF)
+            users = slice(c * CHUNK, (c + 1) * CHUNK)
+            items = slice(h * HALF, (h + 1) * HALF)
+            scores = psum_bank([P, HALF], "scores_%d_%d" % (c, h), (2 * c + h + 1) % BANKS)
+            factors = [
+                (x_codes, x_scale_rows, e_codes, e_plane),
+                (p_codes, p_scales, d_codes, d_scales[:]),
+            ]
+            for n, (user_codes, user_scales, item_codes, item_plane) in enumerate(factors):
+                nc.tensor.matmul_mx(
+                    out=scores[:],
+                    lhsT=user_codes[:, users].bitcast(FP8X4),
+                    lhsT_scale=user_scales[:, users],
+                    rhs=item_codes[:, items].bitcast(FP8X4),
+                    rhs_scale=item_plane[:, items],
+                    start=n == 0,
+                    stop=n == len(factors) - 1,
+                )
             tanh_half = keep.tile([P, HALF], F32, name="tanh_%d_%d" % (c, h))
             result = keep.tile([P, HALF], F32, name="result_%d_%d" % (c, h))
-            nc.scalar.activation(tanh_half[:], scores[c][:, cols], TANH, bias=zero_bias[:], scale=0.5)
+            nc.scalar.activation(tanh_half[:], scores[:], TANH, scale=0.5)
             nc.vector.tensor_scalar(result[:], tanh_half[:], 0.5, 0.5, MULT, ADD)
-            nc.sync.dma_start(out[c * CHUNK : (c + 1) * CHUNK, cols], result[:])
+            nc.sync.dma_start(out[users, items], result[:])
 
         last = CHUNKS - 1
         for c in range(last):
-            gelu(user_tower(c), p_rounded, c, 0, CHUNK)
+            gelu(user_products(c), p_rounded, c)
             quantize_p(c)
-        bank = user_tower(last)
-        gelu(bank, p_rounded, last, 0, CHUNK // 2)
-        finish(0)
+        last_products = user_products(last)
+        gelu(last_products, p_rounded, last, 0, CHUNK // 2)
         leave(0, 0)
-        gelu(bank, p_rounded, last, CHUNK // 2, CHUNK)
+        gelu(last_products, p_rounded, last, CHUNK // 2, CHUNK)
         quantize_p(last)
         leave(0, 1)
         for c in range(1, CHUNKS):
-            finish(c)
-            leave(c, 0)
-            leave(c, 1)
+            for h in range(2):
+                leave(c, h)

@@ -126,23 +126,33 @@ def tile_picked_zneumf_gelu_p_kernel(
 
         w2_rounded = mx_tile([P, PACK * HIDDEN], BF16, "w2_rounded", "rounded_then_x_codes")
         src, dst = rounding_views(w2_raw, w2_rounded)
-        nc.vector.tensor_copy(dst[:, 0], src[:, 0])
-        for t in range(1, PACK):
+        nc.vector.tensor_copy(dst[:, 0:2], src[:, 0:2])
+        for t in range(2, PACK):
             nc.scalar.copy(dst[:, t], src[:, t])
-        x_spread_scales = mx_tile([P, PICKED], U8, "x_spread_scales", "x_spread_scales")
-        nc.vector.tensor_copy(x_spread_scales[:], x_scale_table[:].indirect(offs_sb[:]))
 
-        x_scale_rows = mx_tile([P, PICKED], U8, "x_scale_rows", "w2_raw_then_x_scale_rows")
-        nc.vector.tensor_copy(x_scale_rows[:].bitcast(I32), x_spread_scales[:].bitcast(I32))
-        for r in range(1, QUADRANT_ROWS):
-            nc.scalar.dma_start(
-                x_scale_rows[r:P:QUADRANT, :].bitcast(I32),
-                x_spread_scales[SPREAD * r : P : QUADRANT, :].bitcast(I32),
+        def gather_user_scales(h, tag):
+            picked = mx_tile([P, HALF], U8, "x_spread_scales_%d" % h, tag)
+            nc.vector.tensor_copy(
+                picked[:], x_scale_table[:].indirect(offs_sb[:, h * HALF // LIST_ROWS : (h + 1) * HALF // LIST_ROWS])
             )
+            return picked
 
-        w2_codes = mx_tile([P, HIDDEN], U32, "w2_codes", "x_scale_table_then_w2_codes")
+        x_spread_scales = [gather_user_scales(0, "x_spread_scales_0")]
+        w2_codes = mx_tile([P, HIDDEN], U32, "w2_codes", "w2_codes")
         w2_scales = mx_tile([P, HIDDEN], U8, "w2_scales", "w2_scales")
         quantize(w2_rounded, w2_codes, w2_scales, 0, HIDDEN)
+        x_spread_scales.append(gather_user_scales(1, "w2_raw_then_x_scale_rows"))
+
+        x_scale_rows = mx_tile([P, PICKED], U8, "x_scale_rows", "x_scale_table_then_w2_codes")
+        for h in range(2):
+            nc.vector.tensor_copy(
+                x_scale_rows[:, h * HALF : (h + 1) * HALF].bitcast(I32), x_spread_scales[h][:].bitcast(I32)
+            )
+        for r in range(1, QUADRANT_ROWS):
+            nc.sync.dma_start(
+                x_scale_rows[r:P:QUADRANT, :].bitcast(I32),
+                x_scale_rows[SPREAD * r : P : QUADRANT, :].bitcast(I32),
+            )
 
         last_quarter = PACK - 1
         w1_rounded_last = mx_tile([P, PACK * P], BF16, "w1_rounded_last", "w1_rounded_last")

@@ -180,12 +180,11 @@ def tile_picked_zneumf_gelu_p_kernel(
                 x_table[:].indirect(offs_sb[:, h * HALF // LIST_ROWS : (h + 1) * HALF // LIST_ROWS]),
             )
 
-        d_codes = mx_tile([P, PICKED], U32, "d_codes", "x_table_then_d_codes")
-        d_scales = mx_tile([P, PICKED], U8, "d_scales", "d_scales")
-        for h in range(2):
-            quantize(d_rounded, d_codes, d_scales, h * HALF, (h + 1) * HALF)
+        d_codes = [mx_tile([P, HALF], U32, "d_codes_0", "x_table_then_d_codes")]
+        d_scales = [mx_tile([P, HALF], U8, "d_scales_%d" % h, "d_scales_%d" % h) for h in range(2)]
+        quantize(d_rounded, d_codes[0], d_scales[0], 0, HALF)
 
-        p_rounded = mx_tile([P, PACK * PICKED], BF16, "p_rounded", "p_rounded")
+        p_rounded = [mx_tile([P, PACK * CHUNK], BF16, "p_rounded_%d" % c, "p_rounded_%d" % c) for c in range(CHUNKS)]
         p_codes = mx_tile([P, PICKED], U32, "p_codes", "p_codes")
         p_scales = mx_tile([P, PICKED], U8, "p_scales", "p_scales")
 
@@ -193,23 +192,23 @@ def tile_picked_zneumf_gelu_p_kernel(
             return tower_products(w1_codes, w1_scales, x_codes, x_scale_rows[:], c, (CHUNKS + c + 1) % BANKS)
 
         def quantize_p(c):
-            quantize(p_rounded, p_codes, p_scales, c * CHUNK, (c + 1) * CHUNK)
+            quantize(p_rounded[c], p_codes, p_scales, c * CHUNK, (c + 1) * CHUNK, c * CHUNK)
 
         def leave(c, h):
             users = slice(c * CHUNK, (c + 1) * CHUNK)
             items = slice(h * HALF, (h + 1) * HALF)
             scores = psum_bank([P, HALF], "scores_%d_%d" % (c, h), (2 * c + h + 1) % BANKS)
             factors = [
-                (x_codes, x_scale_rows, e_codes, e_plane),
-                (p_codes, p_scales, d_codes, d_scales[:]),
+                (x_codes, x_scale_rows, e_codes[:, items], e_plane[:, items]),
+                (p_codes, p_scales, d_codes[h][:], d_scales[h][:]),
             ]
             for n, (user_codes, user_scales, item_codes, item_plane) in enumerate(factors):
                 nc.tensor.matmul_mx(
                     out=scores[:],
                     lhsT=user_codes[:, users].bitcast(FP8X4),
                     lhsT_scale=user_scales[:, users],
-                    rhs=item_codes[:, items].bitcast(FP8X4),
-                    rhs_scale=item_plane[:, items],
+                    rhs=item_codes.bitcast(FP8X4),
+                    rhs_scale=item_plane,
                     start=n == 0,
                     stop=n == len(factors) - 1,
                 )
@@ -221,14 +220,17 @@ def tile_picked_zneumf_gelu_p_kernel(
 
         last = CHUNKS - 1
         for c in range(last):
-            gelu(user_products(c), p_rounded, c)
+            gelu(user_products(c), p_rounded[c], 0)
             quantize_p(c)
-        last_products = user_products(last)
-        gelu(last_products, p_rounded, last, 0, CHUNK // 2)
+            if c == 0:
+                d_codes.append(mx_tile([P, HALF], U32, "d_codes_1", "p_rounded_0"))
+                quantize(d_rounded, d_codes[1], d_scales[1], 0, HALF, -HALF)
         leave(0, 0)
-        gelu(last_products, p_rounded, last, CHUNK // 2, CHUNK)
-        quantize_p(last)
         leave(0, 1)
-        for c in range(1, CHUNKS):
+        leave(1, 0)
+        gelu(user_products(last), p_rounded[last], 0)
+        quantize_p(last)
+        leave(1, 1)
+        for c in range(2, CHUNKS):
             for h in range(2):
                 leave(c, h)

@@ -21,7 +21,8 @@ RUN = 4
 QUADRANT = 32
 SCALE_ROWS = 16
 QUADRANT_ROWS = SCALE_ROWS * QUADRANT // P
-SPREAD = P // SCALE_ROWS
+SPREAD = 4
+SPREAD_FROM = 32
 LIST_ROWS = 16
 K = 512
 HIDDEN = 512
@@ -43,6 +44,7 @@ def tile_picked_zneumf_gelu_p_kernel(
     nc = tc.nc
     with ExitStack() as ctx:
         keep = ctx.enter_context(tc.tile_pool(name="keep", bufs=1))
+        shared = ctx.enter_context(tc.tile_pool(name="shared", bufs=1))
         psum = ctx.enter_context(tc.psum_pool(name="psum", bufs=1))
 
         def mx_tile(shape, dtype, name, tag):
@@ -54,9 +56,12 @@ def tile_picked_zneumf_gelu_p_kernel(
         offs_sb = keep.tile([P, PICKED // LIST_ROWS], U16, name="offs_sb")
         cand_sb = keep.tile([P, PICKED // LIST_ROWS], U16, name="cand_sb")
         e_table = mx_tile([P, ITEMS], U32, "e_table", "e_table")
-        x_scale_table = mx_tile([P, USERS], U8, "x_scale_table", "x_scale_table_then_w2_codes")
-        e_scale_table = mx_tile([P, ITEMS], U8, "e_scale_table", "e_scale_table")
-        w2_raw = mx_tile([P, PACK * HIDDEN], F32, "w2_raw", "w2_raw_then_x_scale_rows")
+        x_scale_table = mx_tile([P, USERS], U8, "x_scale_table", "x_scale_table")
+        e_scale_table = shared.tile([P, ITEMS], U8, name="e_scale_table", offset=PACK * PICKED - ITEMS // 2, align_bytes=64)
+        e_scale_rows = mx_tile([P, PICKED], U8, "e_scale_rows", "e_scale_rows")
+        x_scale_rows = mx_tile([P, PICKED], U8, "x_scale_rows", "x_scale_rows")
+        w2_raw = mx_tile([P, PACK * HIDDEN], F32, "w2_raw", "w2_raw")
+        w1_raw = mx_tile([P, PACK * HIDDEN], F32, "w1_raw", "w1_raw")
         zero_in = keep.tile([P, 1], F32, name="zero_in")
         zero_bias = mx_tile([P, 1], F32, "zero_bias", "zero_bias_then_d_rounded")
 
@@ -64,6 +69,8 @@ def tile_picked_zneumf_gelu_p_kernel(
         nc.vector.memset(zero_in[:], 0.0)
         nc.scalar.activation(zero_bias[:], zero_in[:], GELU)
         nc.vector.memset(x_scale_table[:].bitcast(I32), 0)
+        nc.vector.memset(e_scale_rows[:].bitcast(I32), 0)
+        nc.vector.memset(x_scale_rows[:].bitcast(I32), 0)
 
         def load_words(table, words):
             nc.sync.dma_start(table[:].bitcast(I32), words[0].rearrange("p n j -> p (n j)").bitcast(I32))
@@ -71,20 +78,25 @@ def tile_picked_zneumf_gelu_p_kernel(
         def load_weight(raw, w):
             nc.sync.dma_start(raw[:], w.rearrange("(p j) c -> p (j c)", j=PACK))
 
+        def load_scales(table, scales):
+            spread = table[SPREAD_FROM : SPREAD_FROM + SPREAD * SCALE_ROWS : SPREAD, :]
+            nc.sync.dma_start(spread.bitcast(I32), scales[0].bitcast(I32))
+
+        def move_scale_rows(rows, first_row, picked):
+            for r in range(QUADRANT_ROWS):
+                start = SPREAD_FROM + SPREAD * r
+                nc.sync.dma_start(
+                    rows[first_row + r : P : QUADRANT, :].bitcast(I32),
+                    picked[start : start + SPREAD * SCALE_ROWS : SPREAD * QUADRANT_ROWS, :].bitcast(I32),
+                )
+
         load_words(e_table, e_words)
         nc.sync.dma_start(cand_sb[:], cand)
-        for r in range(QUADRANT_ROWS):
-            nc.sync.dma_start(
-                e_scale_table[ITEM_SCALE_ROW + r : P : QUADRANT, :].bitcast(I32),
-                e_scales[0][r:SCALE_ROWS:QUADRANT_ROWS, :].bitcast(I32),
-            )
+        load_scales(e_scale_table, e_scales)
         load_weight(w2_raw, w2)
         nc.sync.dma_start(offs_sb[:], offs)
-        nc.sync.dma_start(x_scale_table[0:P:SPREAD, :].bitcast(I32), x_scales[0].bitcast(I32))
-        w1_raw = mx_tile([P, PACK * HIDDEN], F32, "w1_raw", "w1_raw")
-        x_table = mx_tile([P, USERS], U32, "x_table", "x_table_then_d_codes")
+        load_scales(x_scale_table, x_scales)
         load_weight(w1_raw, w1)
-        load_words(x_table, x_words)
 
         def rounding_views(raw, rounded):
             src = raw[:].rearrange("p (j q t r) -> p t q j r", j=PACK, t=PACK, r=RUN)
@@ -118,41 +130,27 @@ def tile_picked_zneumf_gelu_p_kernel(
             dst = rounded[:, PACK * (c * CHUNK + n0) : PACK * (c * CHUNK + n1)].rearrange("p (n t) -> p n t", t=PACK)
             nc.scalar.activation(dst, products[:, :, n0:n1].rearrange("p t n -> p n t"), GELU)
 
-        e_codes = mx_tile([P, PICKED], U32, "e_codes", "e_codes")
-        e_scale_rows = mx_tile([P, PICKED], U8, "e_scale_rows", "e_scale_rows")
+        e_codes = shared.tile([P, PICKED], U32, name="e_codes", offset=0, align_bytes=64)
+        e_spread_scales = mx_tile([P, PICKED], U8, "e_spread_scales", "e_spread_scales")
+        nc.vector.tensor_copy(e_spread_scales[:], e_scale_table[:].indirect(cand_sb[:]))
+        move_scale_rows(e_scale_rows, ITEM_SCALE_ROW, e_spread_scales)
         nc.vector.tensor_copy(e_codes[:], e_table[:].indirect(cand_sb[:]))
-        nc.vector.tensor_copy(e_scale_rows[:], e_scale_table[:].indirect(cand_sb[:]))
         e_plane = e_scale_rows[ITEM_SCALE_ROW:P, :]
+        x_table = shared.tile([P, USERS], U32, name="x_table", offset=PACK * PICKED, align_bytes=64)
+        load_words(x_table, x_words)
 
         w2_rounded = mx_tile([P, PACK * HIDDEN], BF16, "w2_rounded", "rounded_then_x_codes")
         src, dst = rounding_views(w2_raw, w2_rounded)
         nc.vector.tensor_copy(dst[:, 0:2], src[:, 0:2])
         for t in range(2, PACK):
             nc.scalar.copy(dst[:, t], src[:, t])
+        x_spread_scales = mx_tile([P, PICKED], U8, "x_spread_scales", "x_spread_scales")
+        nc.vector.tensor_copy(x_spread_scales[:], x_scale_table[:].indirect(offs_sb[:]))
+        move_scale_rows(x_scale_rows, 0, x_spread_scales)
 
-        def gather_user_scales(h, tag):
-            picked = mx_tile([P, HALF], U8, "x_spread_scales_%d" % h, tag)
-            nc.vector.tensor_copy(
-                picked[:], x_scale_table[:].indirect(offs_sb[:, h * HALF // LIST_ROWS : (h + 1) * HALF // LIST_ROWS])
-            )
-            return picked
-
-        x_spread_scales = [gather_user_scales(0, "x_spread_scales_0")]
         w2_codes = mx_tile([P, HIDDEN], U32, "w2_codes", "w2_codes")
         w2_scales = mx_tile([P, HIDDEN], U8, "w2_scales", "w2_scales")
         quantize(w2_rounded, w2_codes, w2_scales, 0, HIDDEN)
-        x_spread_scales.append(gather_user_scales(1, "w2_raw_then_x_scale_rows"))
-
-        x_scale_rows = mx_tile([P, PICKED], U8, "x_scale_rows", "x_scale_table_then_w2_codes")
-        for h in range(2):
-            nc.vector.tensor_copy(
-                x_scale_rows[:, h * HALF : (h + 1) * HALF].bitcast(I32), x_spread_scales[h][:].bitcast(I32)
-            )
-        for r in range(1, QUADRANT_ROWS):
-            nc.sync.dma_start(
-                x_scale_rows[r:P:QUADRANT, :].bitcast(I32),
-                x_scale_rows[SPREAD * r : P : QUADRANT, :].bitcast(I32),
-            )
 
         last_quarter = PACK - 1
         w1_rounded_last = mx_tile([P, PACK * P], BF16, "w1_rounded_last", "w1_rounded_last")
@@ -180,7 +178,7 @@ def tile_picked_zneumf_gelu_p_kernel(
                 x_table[:].indirect(offs_sb[:, h * HALF // LIST_ROWS : (h + 1) * HALF // LIST_ROWS]),
             )
 
-        d_codes = [mx_tile([P, HALF], U32, "d_codes_0", "x_table_then_d_codes")]
+        d_codes = [shared.tile([P, HALF], U32, name="d_codes_0", offset=PACK * PICKED, align_bytes=64)]
         d_scales = [mx_tile([P, HALF], U8, "d_scales_%d" % h, "d_scales_%d" % h) for h in range(2)]
         quantize(d_rounded, d_codes[0], d_scales[0], 0, HALF)
 

@@ -69,7 +69,6 @@ def tile_picked_zneumf_gelu_p_kernel(
         nc.vector.memset(zero_in[:], 0.0)
         nc.scalar.activation(zero_bias[:], zero_in[:], GELU)
         nc.vector.memset(x_scale_table[:].bitcast(I32), 0)
-        nc.vector.memset(e_scale_rows[:].bitcast(I32), 0)
         nc.vector.memset(x_scale_rows[:].bitcast(I32), 0)
 
         def load_words(table, words):
@@ -78,24 +77,25 @@ def tile_picked_zneumf_gelu_p_kernel(
         def load_weight(raw, w):
             nc.sync.dma_start(raw[:], w.rearrange("(p j) c -> p (j c)", j=PACK))
 
-        def load_scales(table, scales):
-            spread = table[SPREAD_FROM : SPREAD_FROM + SPREAD * SCALE_ROWS : SPREAD, :]
+        def load_scales(table, scales, first, step):
+            spread = table[first : first + step * (SCALE_ROWS - 1) + 1 : step, :]
             nc.sync.dma_start(spread.bitcast(I32), scales[0].bitcast(I32))
 
-        def move_scale_rows(rows, first_row, picked):
-            for r in range(QUADRANT_ROWS):
-                start = SPREAD_FROM + SPREAD * r
+        def move_scale_rows(rows, first_row, picked, first, step, moved):
+            for r in moved:
+                start = first + step * r
+                stop = start + step * QUADRANT_ROWS * (P // QUADRANT - 1) + 1
                 nc.sync.dma_start(
                     rows[first_row + r : P : QUADRANT, :].bitcast(I32),
-                    picked[start : start + SPREAD * SCALE_ROWS : SPREAD * QUADRANT_ROWS, :].bitcast(I32),
+                    picked[start : stop : step * QUADRANT_ROWS, :].bitcast(I32),
                 )
 
         load_words(e_table, e_words)
         nc.sync.dma_start(cand_sb[:], cand)
-        load_scales(e_scale_table, e_scales)
+        load_scales(e_scale_table, e_scales, ITEM_SCALE_ROW, P // SCALE_ROWS)
         load_weight(w2_raw, w2)
         nc.sync.dma_start(offs_sb[:], offs)
-        load_scales(x_scale_table, x_scales)
+        load_scales(x_scale_table, x_scales, SPREAD_FROM, SPREAD)
         load_weight(w1_raw, w1)
 
         def rounding_views(raw, rounded):
@@ -133,7 +133,8 @@ def tile_picked_zneumf_gelu_p_kernel(
         e_codes = shared.tile([P, PICKED], U32, name="e_codes", offset=0, align_bytes=64)
         e_spread_scales = mx_tile([P, PICKED], U8, "e_spread_scales", "e_spread_scales")
         nc.vector.tensor_copy(e_spread_scales[:], e_scale_table[:].indirect(cand_sb[:]))
-        move_scale_rows(e_scale_rows, ITEM_SCALE_ROW, e_spread_scales)
+        nc.vector.tensor_copy(e_scale_rows[:].bitcast(I32), e_spread_scales[:].bitcast(I32))
+        move_scale_rows(e_scale_rows, ITEM_SCALE_ROW, e_spread_scales, ITEM_SCALE_ROW, P // SCALE_ROWS, range(1, QUADRANT_ROWS))
         nc.vector.tensor_copy(e_codes[:], e_table[:].indirect(cand_sb[:]))
         e_plane = e_scale_rows[ITEM_SCALE_ROW:P, :]
         x_table = shared.tile([P, USERS], U32, name="x_table", offset=PACK * PICKED, align_bytes=64)
@@ -141,12 +142,12 @@ def tile_picked_zneumf_gelu_p_kernel(
 
         w2_rounded = mx_tile([P, PACK * HIDDEN], BF16, "w2_rounded", "rounded_then_x_codes")
         src, dst = rounding_views(w2_raw, w2_rounded)
-        nc.vector.tensor_copy(dst[:, 0:2], src[:, 0:2])
-        for t in range(2, PACK):
+        nc.vector.tensor_copy(dst[:, 0], src[:, 0])
+        for t in range(1, PACK):
             nc.scalar.copy(dst[:, t], src[:, t])
         x_spread_scales = mx_tile([P, PICKED], U8, "x_spread_scales", "x_spread_scales")
         nc.vector.tensor_copy(x_spread_scales[:], x_scale_table[:].indirect(offs_sb[:]))
-        move_scale_rows(x_scale_rows, 0, x_spread_scales)
+        move_scale_rows(x_scale_rows, 0, x_spread_scales, SPREAD_FROM, SPREAD, range(QUADRANT_ROWS))
 
         w2_codes = mx_tile([P, HIDDEN], U32, "w2_codes", "w2_codes")
         w2_scales = mx_tile([P, HIDDEN], U8, "w2_scales", "w2_scales")

@@ -33,6 +33,7 @@ CHUNK = 128
 CHUNKS = PICKED // CHUNK
 HALF = PICKED // 2
 BANKS = 8
+ALIGN = 256
 ITEM_SCALE_ROW = 4
 
 FLOPS = 2 * PICKED * (2 * K * HIDDEN + HIDDEN * PICKED + K * PICKED)
@@ -48,16 +49,16 @@ def tile_picked_zneumf_gelu_p_kernel(
         psum = ctx.enter_context(tc.psum_pool(name="psum", bufs=1))
 
         def mx_tile(shape, dtype, name, tag):
-            return keep.tile(shape, dtype, name=name, tag=tag, align_bytes=64)
+            return keep.tile(shape, dtype, name=name, tag=tag, align_bytes=ALIGN)
 
         def psum_bank(shape, name, bank):
             return psum.tile(shape, F32, name=name, tag="bank%d" % bank)
 
-        offs_sb = keep.tile([P, PICKED // LIST_ROWS], U16, name="offs_sb")
-        cand_sb = keep.tile([P, PICKED // LIST_ROWS], U16, name="cand_sb")
+        offs_sb = keep.tile([P, PICKED // LIST_ROWS], U16, name="offs_sb", align_bytes=ALIGN)
+        cand_sb = keep.tile([P, PICKED // LIST_ROWS], U16, name="cand_sb", align_bytes=ALIGN)
         e_table = mx_tile([P, ITEMS], U32, "e_table", "e_table")
         x_scale_table = mx_tile([P, USERS], U8, "x_scale_table", "x_scale_table")
-        e_scale_table = shared.tile([P, ITEMS], U8, name="e_scale_table", offset=PACK * PICKED - ITEMS // 2, align_bytes=64)
+        e_scale_table = shared.tile([P, ITEMS], U8, name="e_scale_table", offset=PACK * PICKED - ITEMS // 2, align_bytes=ALIGN)
         e_scale_rows = mx_tile([P, PICKED], U8, "e_scale_rows", "e_scale_rows")
         x_scale_rows = mx_tile([P, PICKED], U8, "x_scale_rows", "x_scale_rows")
         w2_raw = mx_tile([P, PACK * HIDDEN], F32, "w2_raw", "w2_raw")
@@ -130,14 +131,14 @@ def tile_picked_zneumf_gelu_p_kernel(
             dst = rounded[:, PACK * (c * CHUNK + n0) : PACK * (c * CHUNK + n1)].rearrange("p (n t) -> p n t", t=PACK)
             nc.scalar.activation(dst, products[:, :, n0:n1].rearrange("p t n -> p n t"), GELU)
 
-        e_codes = shared.tile([P, PICKED], U32, name="e_codes", offset=0, align_bytes=64)
+        e_codes = shared.tile([P, PICKED], U32, name="e_codes", offset=0, align_bytes=ALIGN)
         e_spread_scales = mx_tile([P, PICKED], U8, "e_spread_scales", "e_spread_scales")
         nc.vector.tensor_copy(e_spread_scales[:], e_scale_table[:].indirect(cand_sb[:]))
         nc.vector.tensor_copy(e_scale_rows[:].bitcast(I32), e_spread_scales[:].bitcast(I32))
         move_scale_rows(e_scale_rows, ITEM_SCALE_ROW, e_spread_scales, ITEM_SCALE_ROW, P // SCALE_ROWS, range(1, QUADRANT_ROWS))
         nc.vector.tensor_copy(e_codes[:], e_table[:].indirect(cand_sb[:]))
         e_plane = e_scale_rows[ITEM_SCALE_ROW:P, :]
-        x_table = shared.tile([P, USERS], U32, name="x_table", offset=PACK * PICKED, align_bytes=64)
+        x_table = shared.tile([P, USERS], U32, name="x_table", offset=PACK * PICKED, align_bytes=ALIGN)
         load_words(x_table, x_words)
 
         w2_rounded = mx_tile([P, PACK * HIDDEN], BF16, "w2_rounded", "rounded_then_x_codes")
@@ -179,7 +180,7 @@ def tile_picked_zneumf_gelu_p_kernel(
                 x_table[:].indirect(offs_sb[:, h * HALF // LIST_ROWS : (h + 1) * HALF // LIST_ROWS]),
             )
 
-        d_codes = [shared.tile([P, HALF], U32, name="d_codes_0", offset=PACK * PICKED, align_bytes=64)]
+        d_codes = [shared.tile([P, HALF], U32, name="d_codes_0", offset=PACK * PICKED, align_bytes=ALIGN)]
         d_scales = [mx_tile([P, HALF], U8, "d_scales_%d" % h, "d_scales_%d" % h) for h in range(2)]
         quantize(d_rounded, d_codes[0], d_scales[0], 0, HALF)
 
@@ -212,7 +213,7 @@ def tile_picked_zneumf_gelu_p_kernel(
                     stop=n == len(factors) - 1,
                 )
             tanh_half = keep.tile([P, HALF], F32, name="tanh_%d_%d" % (c, h))
-            result = keep.tile([P, HALF], F32, name="result_%d_%d" % (c, h))
+            result = keep.tile([P, HALF], F32, name="result_%d_%d" % (c, h), align_bytes=ALIGN)
             nc.scalar.activation(tanh_half[:], scores[:], TANH, scale=0.5)
             nc.vector.tensor_scalar(result[:], tanh_half[:], 0.5, 0.5, MULT, ADD)
             nc.sync.dma_start(out[users, items], result[:])

@@ -58,7 +58,7 @@ def tile_picked_zneumf_gelu_p_kernel(
         cand_sb = keep.tile([P, PICKED // LIST_ROWS], U16, name="cand_sb", align_bytes=ALIGN)
         e_table = mx_tile([P, ITEMS], U32, "e_table", "e_table")
         x_scale_table = mx_tile([P, USERS], U8, "x_scale_table", "x_scale_table")
-        e_scale_table = shared.tile([P, ITEMS], U8, name="e_scale_table", offset=PACK * PICKED - ITEMS // 2, align_bytes=ALIGN)
+        e_scale_table = shared.tile([P, ITEMS], U8, name="e_scale_table", offset=PACK * PICKED, align_bytes=ALIGN)
         e_scale_rows = mx_tile([P, PICKED], U8, "e_scale_rows", "e_scale_rows")
         x_scale_rows = mx_tile([P, PICKED], U8, "x_scale_rows", "x_scale_rows")
         w2_raw = mx_tile([P, PACK * HIDDEN], F32, "w2_raw", "w2_raw")
@@ -70,6 +70,7 @@ def tile_picked_zneumf_gelu_p_kernel(
         nc.vector.memset(zero_in[:], 0.0)
         nc.scalar.activation(zero_bias[:], zero_in[:], GELU)
         nc.vector.memset(x_scale_table[:].bitcast(I32), 0)
+        nc.vector.memset(e_scale_rows[:].bitcast(I32), 0)
         nc.vector.memset(x_scale_rows[:].bitcast(I32), 0)
 
         def load_words(table, words):
@@ -92,8 +93,8 @@ def tile_picked_zneumf_gelu_p_kernel(
                 )
 
         load_words(e_table, e_words)
+        load_scales(e_scale_table, e_scales, SPREAD_FROM, SPREAD)
         nc.sync.dma_start(cand_sb[:], cand)
-        load_scales(e_scale_table, e_scales, ITEM_SCALE_ROW, P // SCALE_ROWS)
         load_weight(w2_raw, w2)
         nc.sync.dma_start(offs_sb[:], offs)
         load_scales(x_scale_table, x_scales, SPREAD_FROM, SPREAD)
@@ -134,8 +135,7 @@ def tile_picked_zneumf_gelu_p_kernel(
         e_codes = shared.tile([P, PICKED], U32, name="e_codes", offset=0, align_bytes=ALIGN)
         e_spread_scales = mx_tile([P, PICKED], U8, "e_spread_scales", "e_spread_scales")
         nc.vector.tensor_copy(e_spread_scales[:], e_scale_table[:].indirect(cand_sb[:]))
-        nc.vector.tensor_copy(e_scale_rows[:].bitcast(I32), e_spread_scales[:].bitcast(I32))
-        move_scale_rows(e_scale_rows, ITEM_SCALE_ROW, e_spread_scales, ITEM_SCALE_ROW, P // SCALE_ROWS, range(1, QUADRANT_ROWS))
+        move_scale_rows(e_scale_rows, ITEM_SCALE_ROW, e_spread_scales, SPREAD_FROM, SPREAD, range(QUADRANT_ROWS))
         nc.vector.tensor_copy(e_codes[:], e_table[:].indirect(cand_sb[:]))
         e_plane = e_scale_rows[ITEM_SCALE_ROW:P, :]
         x_table = shared.tile([P, USERS], U32, name="x_table", offset=PACK * PICKED, align_bytes=ALIGN)
@@ -174,10 +174,10 @@ def tile_picked_zneumf_gelu_p_kernel(
         quantize(w1_rounded, w1_codes, w1_scales, 2 * P, last_quarter * P)
 
         x_codes = mx_tile([P, PICKED], U32, "x_codes", "rounded_then_x_codes")
-        for h in range(2):
+        for c in range(CHUNKS):
             nc.vector.tensor_copy(
-                x_codes[:, h * HALF : (h + 1) * HALF],
-                x_table[:].indirect(offs_sb[:, h * HALF // LIST_ROWS : (h + 1) * HALF // LIST_ROWS]),
+                x_codes[:, c * CHUNK : (c + 1) * CHUNK],
+                x_table[:].indirect(offs_sb[:, c * CHUNK // LIST_ROWS : (c + 1) * CHUNK // LIST_ROWS]),
             )
 
         d_codes = [shared.tile([P, HALF], U32, name="d_codes_0", offset=PACK * PICKED, align_bytes=ALIGN)]

@@ -218,19 +218,12 @@ def tile_picked_zneumf_gelu_p_kernel(
             nc.vector.tensor_scalar(result[:], tanh_half[:], 0.5, 0.5, MULT, ADD)
             nc.sync.dma_start(out[users, items], result[:])
 
-        last = CHUNKS - 1
-        for c in range(last):
+        for c in range(CHUNKS):
             gelu(user_products(c), p_rounded[c], 0)
             quantize_p(c)
             if c == 0:
                 d_codes.append(mx_tile([P, HALF], U32, "d_codes_1", "p_rounded_0"))
                 quantize(d_rounded, d_codes[1], d_scales[1], 0, HALF, -HALF)
-        leave(0, 0)
-        leave(0, 1)
-        leave(1, 0)
-        gelu(user_products(last), p_rounded[last], 0)
-        quantize_p(last)
-        leave(1, 1)
-        for c in range(2, CHUNKS):
+        for c in range(CHUNKS):
             for h in range(2):
                 leave(c, h)

@@ -154,10 +154,11 @@ def tile_picked_zneumf_gelu_p_kernel(
         w2_scales = mx_tile([P, HIDDEN], U8, "w2_scales", "w2_scales")
         quantize(w2_rounded, w2_codes, w2_scales, 0, HIDDEN)
 
-        last_quarter = PACK - 1
-        w1_rounded_last = mx_tile([P, PACK * P], BF16, "w1_rounded_last", "w1_rounded_last")
+        last_quarter = 2
+        w1_rounded_last = mx_tile([P, 2 * PACK * P], BF16, "w1_rounded_last", "w1_rounded_last")
         src, dst = rounding_views(w1_raw, w1_rounded_last)
-        nc.scalar.activation(dst[:, 0], src[:, last_quarter], IDENTITY, bias=zero_bias[:])
+        nc.scalar.copy(dst[:, 0], src[:, 2])
+        nc.scalar.activation(dst[:, 1], src[:, 3], IDENTITY, bias=zero_bias[:])
 
         d_rounded = mx_tile([P, PACK * PICKED], BF16, "d_rounded", "zero_bias_then_d_rounded")
         for c in range(CHUNKS):
@@ -168,10 +169,8 @@ def tile_picked_zneumf_gelu_p_kernel(
         w1_scales = mx_tile([P, HIDDEN], U8, "w1_scales", "w1_scales")
         src, dst = rounding_views(w1_raw, w1_rounded)
         nc.vector.tensor_copy(dst[:, 0:2], src[:, 0:2])
-        nc.vector.tensor_copy(dst[:, 2], src[:, 2])
         quantize(w1_rounded_last, w1_codes, w1_scales, last_quarter * P, HIDDEN, last_quarter * P)
         quantize(w1_rounded, w1_codes, w1_scales, 0, 2 * P)
-        quantize(w1_rounded, w1_codes, w1_scales, 2 * P, last_quarter * P)
 
         x_codes = mx_tile([P, PICKED], U32, "x_codes", "rounded_then_x_codes")
         for c in range(CHUNKS):

@@ -154,11 +154,10 @@ def tile_picked_zneumf_gelu_p_kernel(
         w2_scales = mx_tile([P, HIDDEN], U8, "w2_scales", "w2_scales")
         quantize(w2_rounded, w2_codes, w2_scales, 0, HIDDEN)
 
-        last_quarter = 2
-        w1_rounded_last = mx_tile([P, 2 * PACK * P], BF16, "w1_rounded_last", "w1_rounded_last")
+        last_quarter = PACK - 1
+        w1_rounded_last = mx_tile([P, PACK * P], BF16, "w1_rounded_last", "w1_rounded_last")
         src, dst = rounding_views(w1_raw, w1_rounded_last)
-        nc.scalar.copy(dst[:, 0], src[:, 2])
-        nc.scalar.activation(dst[:, 1], src[:, 3], IDENTITY, bias=zero_bias[:])
+        nc.scalar.activation(dst[:, 0], src[:, last_quarter], IDENTITY, bias=zero_bias[:])
 
         d_rounded = mx_tile([P, PACK * PICKED], BF16, "d_rounded", "zero_bias_then_d_rounded")
         for c in range(CHUNKS):
@@ -169,8 +168,10 @@ def tile_picked_zneumf_gelu_p_kernel(
         w1_scales = mx_tile([P, HIDDEN], U8, "w1_scales", "w1_scales")
         src, dst = rounding_views(w1_raw, w1_rounded)
         nc.vector.tensor_copy(dst[:, 0:2], src[:, 0:2])
+        nc.vector.tensor_copy(dst[:, 2], src[:, 2])
         quantize(w1_rounded_last, w1_codes, w1_scales, last_quarter * P, HIDDEN, last_quarter * P)
         quantize(w1_rounded, w1_codes, w1_scales, 0, 2 * P)
+        quantize(w1_rounded, w1_codes, w1_scales, 2 * P, last_quarter * P)
 
         x_codes = mx_tile([P, PICKED], U32, "x_codes", "rounded_then_x_codes")
         for c in range(CHUNKS):
@@ -190,13 +191,35 @@ def tile_picked_zneumf_gelu_p_kernel(
         def user_products(c):
             return tower_products(w1_codes, w1_scales, x_codes, x_scale_rows[:], c, (CHUNKS + c + 1) % BANKS)
 
+        def first_user_step():
+            apart = mx_tile([P, 2, 2 * CHUNK], BF16, "p_apart", "p_apart")
+            for h in range(2):
+                products = psum_bank([P, 2, CHUNK], "first_products_%d" % h, CHUNKS + h)
+                for u in range(2):
+                    quarter = slice((2 * h + u) * P, (2 * h + u + 1) * P)
+                    nc.tensor.matmul_mx(
+                        out=products[:, u, :],
+                        lhsT=w1_codes[:, quarter].bitcast(FP8X4),
+                        lhsT_scale=w1_scales[:, quarter],
+                        rhs=x_codes[:, 0:CHUNK].bitcast(FP8X4),
+                        rhs_scale=x_scale_rows[:, 0:CHUNK],
+                        start=True,
+                        stop=True,
+                    )
+                dst = apart[:, h, :].rearrange("p (n u) -> p n u", u=2)
+                nc.scalar.activation(dst, products[:].rearrange("p u n -> p n u"), GELU)
+            nc.vector.tensor_copy(
+                p_rounded[0][:].bitcast(F32).rearrange("p (n h) -> p n h", h=2),
+                apart[:].bitcast(F32).rearrange("p h n -> p n h"),
+            )
+
         def quantize_p(c):
             quantize(p_rounded[c], p_codes, p_scales, c * CHUNK, (c + 1) * CHUNK, c * CHUNK)
 
-        def leave(c, h):
+        def leave(c, h, bank):
             users = slice(c * CHUNK, (c + 1) * CHUNK)
             items = slice(h * HALF, (h + 1) * HALF)
-            scores = psum_bank([P, HALF], "scores_%d_%d" % (c, h), (2 * c + h + 1) % BANKS)
+            scores = psum_bank([P, HALF], "scores_%d_%d" % (c, h), bank)
             factors = [
                 (x_codes, x_scale_rows, e_codes[:, items], e_plane[:, items]),
                 (p_codes, p_scales, d_codes[h][:], d_scales[h][:]),
@@ -218,11 +241,14 @@ def tile_picked_zneumf_gelu_p_kernel(
             nc.sync.dma_start(out[users, items], result[:])
 
         for c in range(CHUNKS):
-            gelu(user_products(c), p_rounded[c], 0)
-            quantize_p(c)
             if c == 0:
+                first_user_step()
+            else:
+                gelu(user_products(c), p_rounded[c], 0)
+            quantize_p(c)
+            if c == 1:
                 d_codes.append(mx_tile([P, HALF], U32, "d_codes_1", "p_rounded_0"))
                 quantize(d_rounded, d_codes[1], d_scales[1], 0, HALF, -HALF)
-        for c in range(CHUNKS):
-            for h in range(2):
-                leave(c, h)
+        steps = [(c, h) for h in range(2) for c in range(2)] + [(c, h) for c in range(2, CHUNKS) for h in range(2)]
+        for n, (c, h) in enumerate(steps):
+            leave(c, h, (n + 1) % BANKS)

@@ -152,7 +152,19 @@ def tile_picked_zneumf_gelu_p_kernel(
 
         w2_codes = mx_tile([P, HIDDEN], U32, "w2_codes", "w2_codes")
         w2_scales = mx_tile([P, HIDDEN], U8, "w2_scales", "w2_scales")
-        quantize(w2_rounded, w2_codes, w2_scales, 0, HIDDEN)
+        quantize(w2_rounded, w2_codes, w2_scales, 0, HIDDEN // 2)
+        warm = psum_bank([P, HALF], "warm", BANKS - 1)
+        for n in range(3):
+            nc.tensor.matmul_mx(
+                out=warm[:],
+                lhsT=w2_codes[:, 0:P].bitcast(FP8X4),
+                lhsT_scale=w2_scales[:, 0:P],
+                rhs=w2_codes[:, 0:HALF].bitcast(FP8X4),
+                rhs_scale=w2_scales[:, 0:HALF],
+                start=True,
+                stop=True,
+            )
+        quantize(w2_rounded, w2_codes, w2_scales, HIDDEN // 2, HIDDEN)
 
         last_quarter = PACK - 1
         w1_rounded_last = mx_tile([P, PACK * P], BF16, "w1_rounded_last", "w1_rounded_last")

@@ -153,17 +153,6 @@ def tile_picked_zneumf_gelu_p_kernel(
         w2_codes = mx_tile([P, HIDDEN], U32, "w2_codes", "w2_codes")
         w2_scales = mx_tile([P, HIDDEN], U8, "w2_scales", "w2_scales")
         quantize(w2_rounded, w2_codes, w2_scales, 0, HIDDEN // 2)
-        warm = psum_bank([P, HALF], "warm", BANKS - 1)
-        for n in range(3):
-            nc.tensor.matmul_mx(
-                out=warm[:],
-                lhsT=w2_codes[:, 0:P].bitcast(FP8X4),
-                lhsT_scale=w2_scales[:, 0:P],
-                rhs=w2_codes[:, 0:HALF].bitcast(FP8X4),
-                rhs_scale=w2_scales[:, 0:HALF],
-                start=True,
-                stop=True,
-            )
         quantize(w2_rounded, w2_codes, w2_scales, HIDDEN // 2, HIDDEN)
 
         last_quarter = PACK - 1

@@ -181,9 +181,9 @@ def tile_picked_zneumf_gelu_p_kernel(
                 x_table[:].indirect(offs_sb[:, c * CHUNK // LIST_ROWS : (c + 1) * CHUNK // LIST_ROWS]),
             )
 
-        d_codes = [shared.tile([P, HALF], U32, name="d_codes_0", offset=PACK * PICKED, align_bytes=ALIGN)]
+        d_codes = {1: mx_tile([P, HALF], U32, "d_codes_1", "d_codes_1")}
         d_scales = [mx_tile([P, HALF], U8, "d_scales_%d" % h, "d_scales_%d" % h) for h in range(2)]
-        quantize(d_rounded, d_codes[0], d_scales[0], 0, HALF)
+        quantize(d_rounded, d_codes[1], d_scales[1], 0, HALF, -HALF)
 
         p_rounded = [mx_tile([P, PACK * CHUNK], BF16, "p_rounded_%d" % c, "p_rounded_%d" % c) for c in range(CHUNKS)]
         p_codes = mx_tile([P, PICKED], U32, "p_codes", "p_codes")
@@ -248,8 +248,8 @@ def tile_picked_zneumf_gelu_p_kernel(
                 gelu(user_products(c), p_rounded[c], 0)
             quantize_p(c)
             if c == 1:
-                d_codes.append(mx_tile([P, HALF], U32, "d_codes_1", "p_rounded_0"))
-                quantize(d_rounded, d_codes[1], d_scales[1], 0, HALF, -HALF)
-        steps = [(c, h) for h in range(2) for c in range(2)] + [(c, h) for c in range(2, CHUNKS) for h in range(2)]
+                d_codes[0] = mx_tile([P, HALF], U32, "d_codes_0", "p_rounded_0")
+                quantize(d_rounded, d_codes[0], d_scales[0], 0, HALF)
+        steps = [(c, h) for h in (1, 0) for c in range(2)] + [(c, h) for c in range(2, CHUNKS) for h in range(2)]
         for n, (c, h) in enumerate(steps):
             leave(c, h, (n + 1) % BANKS)

@@ -160,8 +160,25 @@ def tile_picked_zneumf_gelu_p_kernel(
         src, dst = rounding_views(w1_raw, w1_rounded_last)
         nc.scalar.activation(dst[:, 0], src[:, last_quarter], IDENTITY, bias=zero_bias[:])
 
-        d_rounded = mx_tile([P, PACK * PICKED], BF16, "d_rounded", "zero_bias_then_d_rounded")
-        for c in range(CHUNKS):
+        d_rounded = mx_tile([P, PACK * PICKED], BF16, "d_rounded", "d_rounded")
+        d_apart = mx_tile([P, 2, 2 * CHUNK], BF16, "d_apart", "zero_bias_then_d_rounded")
+        for h in range(2):
+            products = psum_bank([P, 2, CHUNK], "first_item_products_%d" % h, CHUNKS + h)
+            for u in range(2):
+                quarter = slice((2 * h + u) * P, (2 * h + u + 1) * P)
+                nc.tensor.matmul_mx(
+                    out=products[:, u, :],
+                    lhsT=w2_codes[:, quarter].bitcast(FP8X4),
+                    lhsT_scale=w2_scales[:, quarter],
+                    rhs=e_codes[:, 0:CHUNK].bitcast(FP8X4),
+                    rhs_scale=e_plane[:, 0:CHUNK],
+                    start=True,
+                    stop=True,
+                )
+            nc.scalar.activation(
+                d_apart[:, h, :].rearrange("p (n u) -> p n u", u=2), products[:].rearrange("p u n -> p n u"), GELU
+            )
+        for c in range(1, CHUNKS):
             gelu(tower_products(w2_codes, w2_scales, e_codes, e_plane, c, c), d_rounded, c)
 
         w1_rounded = mx_tile([P, last_quarter * PACK * P], BF16, "w1_rounded", "rounded_then_x_codes")
@@ -185,6 +202,10 @@ def tile_picked_zneumf_gelu_p_kernel(
         d_scales = [mx_tile([P, HALF], U8, "d_scales_%d" % h, "d_scales_%d" % h) for h in range(2)]
         quantize(d_rounded, d_codes[1], d_scales[1], 0, HALF, -HALF)
 
+        nc.vector.tensor_copy(
+            d_rounded[:, 0 : PACK * CHUNK].bitcast(F32).rearrange("p (n h) -> p n h", h=2),
+            d_apart[:].bitcast(F32).rearrange("p h n -> p n h"),
+        )
         p_rounded = [mx_tile([P, PACK * CHUNK], BF16, "p_rounded_%d" % c, "p_rounded_%d" % c) for c in range(CHUNKS)]
         p_codes = mx_tile([P, PICKED], U32, "p_codes", "p_codes")
         p_scales = mx_tile([P, PICKED], U8, "p_scales", "p_scales")

from contextlib import ExitStack

import concourse.mybir as mybir

F32 = mybir.dt.float32
BF16 = mybir.dt.bfloat16
I32 = mybir.dt.int32
U32 = mybir.dt.uint32
U16 = mybir.dt.uint16
U8 = mybir.dt.uint8
FP8X4 = mybir.dt.float8_e4m3fn_x4
GELU = mybir.ActivationFunctionType.Gelu_apprx_tanh
IDENTITY = mybir.ActivationFunctionType.Identity
TANH = mybir.ActivationFunctionType.Tanh
MULT = mybir.AluOpType.mult
ADD = mybir.AluOpType.add

P = 128
PACK = 4
RUN = 4
QUADRANT = 32
SCALE_ROWS = 16
QUADRANT_ROWS = SCALE_ROWS * QUADRANT // P
SPREAD = 4
SPREAD_FROM = 32
LIST_ROWS = 16
K = 512
HIDDEN = 512
USERS = 2048
ITEMS = 1024
PICKED = 512
CHUNK = 128
CHUNKS = PICKED // CHUNK
HALF = PICKED // 2
BANKS = 8
ALIGN = 256
ITEM_SCALE_ROW = 4

FLOPS = 2 * PICKED * (2 * K * HIDDEN + HIDDEN * PICKED + K * PICKED)


def tile_picked_zneumf_gelu_p_kernel(
    tc, x_words, x_scales, e_words, e_scales, w1, w2, offs, cand, out
):
    nc = tc.nc
    with ExitStack() as ctx:
        keep = ctx.enter_context(tc.tile_pool(name="keep", bufs=1))
        shared = ctx.enter_context(tc.tile_pool(name="shared", bufs=1))
        psum = ctx.enter_context(tc.psum_pool(name="psum", bufs=1))

        def mx_tile(shape, dtype, name, tag):
            return keep.tile(shape, dtype, name=name, tag=tag, align_bytes=ALIGN)

        def psum_bank(shape, name, bank):
            return psum.tile(shape, F32, name=name, tag="bank%d" % bank)

        offs_sb = keep.tile([P, PICKED // LIST_ROWS], U16, name="offs_sb", align_bytes=ALIGN)
        cand_sb = keep.tile([P, PICKED // LIST_ROWS], U16, name="cand_sb", align_bytes=ALIGN)
        e_table = mx_tile([P, ITEMS], U32, "e_table", "e_table")
        x_scale_table = mx_tile([P, USERS], U8, "x_scale_table", "x_scale_table")
        e_scale_table = shared.tile([P, ITEMS], U8, name="e_scale_table", offset=PACK * PICKED, align_bytes=ALIGN)
        e_scale_rows = mx_tile([P, PICKED], U8, "e_scale_rows", "e_scale_rows")
        x_scale_rows = mx_tile([P, PICKED], U8, "x_scale_rows", "x_scale_rows")
        w2_raw = mx_tile([P, PACK * HIDDEN], F32, "w2_raw", "w2_raw")
        w1_raw = mx_tile([P, PACK * HIDDEN], F32, "w1_raw", "w1_raw")
        zero_in = keep.tile([P, 1], F32, name="zero_in")
        zero_bias = mx_tile([P, 1], F32, "zero_bias", "zero_bias_then_d_rounded")

        nc.vector.memset(e_scale_table[:].bitcast(I32), 0)
        nc.vector.memset(zero_in[:], 0.0)
        nc.scalar.activation(zero_bias[:], zero_in[:], GELU)
        nc.vector.memset(x_scale_table[:].bitcast(I32), 0)
        nc.vector.memset(e_scale_rows[:].bitcast(I32), 0)
        nc.vector.memset(x_scale_rows[:].bitcast(I32), 0)

        def load_words(table, words):
            nc.sync.dma_start(table[:].bitcast(I32), words[0].rearrange("p n j -> p (n j)").bitcast(I32))

        def load_weight(raw, w):
            nc.sync.dma_start(raw[:], w.rearrange("(p j) c -> p (j c)", j=PACK))

        def load_scales(table, scales, first, step):
            spread = table[first : first + step * (SCALE_ROWS - 1) + 1 : step, :]
            nc.sync.dma_start(spread.bitcast(I32), scales[0].bitcast(I32))

        def move_scale_rows(rows, first_row, picked, first, step, moved):
            for r in moved:
                start = first + step * r
                stop = start + step * QUADRANT_ROWS * (P // QUADRANT - 1) + 1
                nc.sync.dma_start(
                    rows[first_row + r : P : QUADRANT, :].bitcast(I32),
                    picked[start : stop : step * QUADRANT_ROWS, :].bitcast(I32),
                )

        load_words(e_table, e_words)
        load_scales(e_scale_table, e_scales, SPREAD_FROM, SPREAD)
        nc.sync.dma_start(cand_sb[:], cand)
        load_weight(w2_raw, w2)
        nc.sync.dma_start(offs_sb[:], offs)
        load_scales(x_scale_table, x_scales, SPREAD_FROM, SPREAD)
        load_weight(w1_raw, w1)

        def rounding_views(raw, rounded):
            src = raw[:].rearrange("p (j q t r) -> p t q j r", j=PACK, t=PACK, r=RUN)
            dst = rounded[:].rearrange("p (t q r j) -> p t q j r", j=PACK, q=P // RUN, r=RUN)
            return src, dst

        def quantize(rounded, codes, scales, c0, c1, rounded_from=0):
            nc.vector.quantize_mx(
                out=codes[:, c0:c1].bitcast(FP8X4),
                scales=scales[:, c0:c1],
                in_=rounded[:, PACK * (c0 - rounded_from) : PACK * (c1 - rounded_from)],
            )

        def tower_products(w_codes, w_scales, codes, scales, c, bank):
            cols = slice(c * CHUNK, (c + 1) * CHUNK)
            products = psum_bank([P, PACK, CHUNK], "products", bank)
            for t in range(PACK):
                quarter = slice(t * P, (t + 1) * P)
                nc.tensor.matmul_mx(
                    out=products[:, t, :],
                    lhsT=w_codes[:, quarter].bitcast(FP8X4),
                    lhsT_scale=w_scales[:, quarter],
                    rhs=codes[:, cols].bitcast(FP8X4),
                    rhs_scale=scales[:, cols],
                    start=True,
                    stop=True,
                )
            return products

        def gelu(products, rounded, c, n0=0, n1=CHUNK):
            dst = rounded[:, PACK * (c * CHUNK + n0) : PACK * (c * CHUNK + n1)].rearrange("p (n t) -> p n t", t=PACK)
            nc.scalar.activation(dst, products[:, :, n0:n1].rearrange("p t n -> p n t"), GELU)

        e_codes = shared.tile([P, PICKED], U32, name="e_codes", offset=0, align_bytes=ALIGN)
        e_spread_scales = mx_tile([P, PICKED], U8, "e_spread_scales", "e_spread_scales")
        nc.vector.tensor_copy(e_spread_scales[:], e_scale_table[:].indirect(cand_sb[:]))
        move_scale_rows(e_scale_rows, ITEM_SCALE_ROW, e_spread_scales, SPREAD_FROM, SPREAD, range(QUADRANT_ROWS))
        nc.vector.tensor_copy(e_codes[:], e_table[:].indirect(cand_sb[:]))
        e_plane = e_scale_rows[ITEM_SCALE_ROW:P, :]
        x_table = shared.tile([P, USERS], U32, name="x_table", offset=PACK * PICKED, align_bytes=ALIGN)
        load_words(x_table, x_words)

        w2_rounded = mx_tile([P, PACK * HIDDEN], BF16, "w2_rounded", "rounded_then_x_codes")
        src, dst = rounding_views(w2_raw, w2_rounded)
        nc.vector.tensor_copy(dst[:, 0], src[:, 0])
        for t in range(1, PACK):
            nc.scalar.copy(dst[:, t], src[:, t])
        x_spread_scales = mx_tile([P, PICKED], U8, "x_spread_scales", "x_spread_scales")
        nc.vector.tensor_copy(x_spread_scales[:], x_scale_table[:].indirect(offs_sb[:]))
        move_scale_rows(x_scale_rows, 0, x_spread_scales, SPREAD_FROM, SPREAD, range(QUADRANT_ROWS))

        w2_codes = mx_tile([P, HIDDEN], U32, "w2_codes", "w2_codes")
        w2_scales = mx_tile([P, HIDDEN], U8, "w2_scales", "w2_scales")
        quantize(w2_rounded, w2_codes, w2_scales, 0, HIDDEN // 2)
        quantize(w2_rounded, w2_codes, w2_scales, HIDDEN // 2, HIDDEN)

        last_quarter = PACK - 1
        w1_rounded_last = mx_tile([P, PACK * P], BF16, "w1_rounded_last", "w1_rounded_last")
        src, dst = rounding_views(w1_raw, w1_rounded_last)
        nc.scalar.activation(dst[:, 0], src[:, last_quarter], IDENTITY, bias=zero_bias[:])

        d_rounded = mx_tile([P, PACK * PICKED], BF16, "d_rounded", "d_rounded")
        d_apart = mx_tile([P, 2, 2 * CHUNK], BF16, "d_apart", "zero_bias_then_d_rounded")
        for h in range(2):
            products = psum_bank([P, 2, CHUNK], "first_item_products_%d" % h, CHUNKS + h)
            for u in range(2):
                quarter = slice((2 * h + u) * P, (2 * h + u + 1) * P)
                nc.tensor.matmul_mx(
                    out=products[:, u, :],
                    lhsT=w2_codes[:, quarter].bitcast(FP8X4),
                    lhsT_scale=w2_scales[:, quarter],
                    rhs=e_codes[:, 0:CHUNK].bitcast(FP8X4),
                    rhs_scale=e_plane[:, 0:CHUNK],
                    start=True,
                    stop=True,
                )
            nc.scalar.activation(
                d_apart[:, h, :].rearrange("p (n u) -> p n u", u=2), products[:].rearrange("p u n -> p n u"), GELU
            )
        for c in range(1, CHUNKS):
            gelu(tower_products(w2_codes, w2_scales, e_codes, e_plane, c, c), d_rounded, c)

        w1_rounded = mx_tile([P, last_quarter * PACK * P], BF16, "w1_rounded", "rounded_then_x_codes")
        w1_codes = mx_tile([P, HIDDEN], U32, "w1_codes", "w1_codes")
        w1_scales = mx_tile([P, HIDDEN], U8, "w1_scales", "w1_scales")
        src, dst = rounding_views(w1_raw, w1_rounded)
        nc.vector.tensor_copy(dst[:, 0:2], src[:, 0:2])
        nc.vector.tensor_copy(dst[:, 2], src[:, 2])
        quantize(w1_rounded_last, w1_codes, w1_scales, last_quarter * P, HIDDEN, last_quarter * P)
        quantize(w1_rounded, w1_codes, w1_scales, 0, 2 * P)
        quantize(w1_rounded, w1_codes, w1_scales, 2 * P, last_quarter * P)

        x_codes = mx_tile([P, PICKED], U32, "x_codes", "rounded_then_x_codes")
        for c in range(CHUNKS):
            nc.vector.tensor_copy(
                x_codes[:, c * CHUNK : (c + 1) * CHUNK],
                x_table[:].indirect(offs_sb[:, c * CHUNK // LIST_ROWS : (c + 1) * CHUNK // LIST_ROWS]),
            )

        d_codes = {1: mx_tile([P, HALF], U32, "d_codes_1", "d_codes_1")}
        d_scales = [mx_tile([P, HALF], U8, "d_scales_%d" % h, "d_scales_%d" % h) for h in range(2)]
        quantize(d_rounded, d_codes[1], d_scales[1], 0, HALF, -HALF)

        nc.vector.tensor_copy(
            d_rounded[:, 0 : PACK * CHUNK].bitcast(F32).rearrange("p (n h) -> p n h", h=2),
            d_apart[:].bitcast(F32).rearrange("p h n -> p n h"),
        )
        p_rounded = [mx_tile([P, PACK * CHUNK], BF16, "p_rounded_%d" % c, "p_rounded_%d" % c) for c in range(CHUNKS)]
        p_codes = mx_tile([P, PICKED], U32, "p_codes", "p_codes")
        p_scales = mx_tile([P, PICKED], U8, "p_scales", "p_scales")

        def user_products(c):
            return tower_products(w1_codes, w1_scales, x_codes, x_scale_rows[:], c, (CHUNKS + c + 1) % BANKS)

        def first_user_step():
            apart = mx_tile([P, 2, 2 * CHUNK], BF16, "p_apart", "p_apart")
            for h in range(2):
                products = psum_bank([P, 2, CHUNK], "first_products_%d" % h, CHUNKS + h)
                for u in range(2):
                    quarter = slice((2 * h + u) * P, (2 * h + u + 1) * P)
                    nc.tensor.matmul_mx(
                        out=products[:, u, :],
                        lhsT=w1_codes[:, quarter].bitcast(FP8X4),
                        lhsT_scale=w1_scales[:, quarter],
                        rhs=x_codes[:, 0:CHUNK].bitcast(FP8X4),
                        rhs_scale=x_scale_rows[:, 0:CHUNK],
                        start=True,
                        stop=True,
                    )
                dst = apart[:, h, :].rearrange("p (n u) -> p n u", u=2)
                nc.scalar.activation(dst, products[:].rearrange("p u n -> p n u"), GELU)
            nc.vector.tensor_copy(
                p_rounded[0][:].bitcast(F32).rearrange("p (n h) -> p n h", h=2),
                apart[:].bitcast(F32).rearrange("p h n -> p n h"),
            )

        def quantize_p(c):
            quantize(p_rounded[c], p_codes, p_scales, c * CHUNK, (c + 1) * CHUNK, c * CHUNK)

        def leave(c, h, bank):
            users = slice(c * CHUNK, (c + 1) * CHUNK)
            items = slice(h * HALF, (h + 1) * HALF)
            scores = psum_bank([P, HALF], "scores_%d_%d" % (c, h), bank)
            factors = [
                (x_codes, x_scale_rows, e_codes[:, items], e_plane[:, items]),
                (p_codes, p_scales, d_codes[h][:], d_scales[h][:]),
            ]
            for n, (user_codes, user_scales, item_codes, item_plane) in enumerate(factors):
                nc.tensor.matmul_mx(
                    out=scores[:],
                    lhsT=user_codes[:, users].bitcast(FP8X4),
                    lhsT_scale=user_scales[:, users],
                    rhs=item_codes.bitcast(FP8X4),
                    rhs_scale=item_plane,
                    start=n == 0,
                    stop=n == len(factors) - 1,
                )
            tanh_half = keep.tile([P, HALF], F32, name="tanh_%d_%d" % (c, h))
            result = keep.tile([P, HALF], F32, name="result_%d_%d" % (c, h), align_bytes=ALIGN)
            nc.scalar.activation(tanh_half[:], scores[:], TANH, scale=0.5)
            nc.vector.tensor_scalar(result[:], tanh_half[:], 0.5, 0.5, MULT, ADD)
            nc.sync.dma_start(out[users, items], result[:])

        for c in range(CHUNKS):
            if c == 0:
                first_user_step()
            else:
                gelu(user_products(c), p_rounded[c], 0)
            quantize_p(c)
            if c == 1:
                d_codes[0] = mx_tile([P, HALF], U32, "d_codes_0", "p_rounded_0")
                quantize(d_rounded, d_codes[0], d_scales[0], 0, HALF)
        steps = [(c, h) for h in (1, 0) for c in range(2)] + [(c, h) for c in range(2, CHUNKS) for h in range(2)]
        for n, (c, h) in enumerate(steps):
            leave(c, h, (n + 1) % BANKS)
